import numpy as np
import ml_dtypes


def mxq(x, axis, fmt="e4m3"):
    dtype, down = {"e4m3": (ml_dtypes.float8_e4m3fn, 7), "e5m2": (ml_dtypes.float8_e5m2, 14)}[fmt]
    v = np.moveaxis(np.asarray(x, np.float32).astype(ml_dtypes.bfloat16).astype(np.float64), axis, -1)
    blocks = v.reshape(v.shape[:-1] + (-1, 32))
    amax = np.abs(blocks).max(-1, keepdims=True)
    byte = np.maximum(np.where(amax > 0, np.frexp(amax)[1] - 1 + 127, 0) - down, 1)
    scale = np.exp2(byte - 127.0)
    codes = (blocks / scale).astype(np.float32).astype(dtype).astype(np.float64)
    return np.moveaxis((codes * scale).reshape(v.shape), -1, axis)


WIDE = False


def mx_kscale(k):
    if not WIDE:
        return np.ones(k)
    levels = np.array([10, -10, 5, -5, 0])
    if k % 512:
        return np.exp2(np.random.permutation(np.resize(levels, k // 32))).repeat(32)
    a = np.empty((k // 512, 16))
    for p in range(k // 512):
        a[p, :8] = np.random.permutation(np.resize(levels, 8))
        for g in range(8):
            far = levels[np.abs(levels - a[p, g]) >= 10]
            a[p, g + 8] = far[np.random.randint(len(far))]
    return np.exp2(a.ravel()).repeat(32)


def f64(x):
    return np.asarray(x).astype(np.float64)


E2M1 = np.array([0.0, 0.5, 1.0, 1.5, 2.0, 3.0, 4.0, 6.0, -0.0, -0.5, -1.0, -1.5, -2.0, -3.0, -4.0, -6.0])


def pack_weight(w, fmt):
    k, n = w.shape
    w = f64(np.asarray(w, np.float32).astype(ml_dtypes.bfloat16)).reshape(k // 32, 32, n)
    amax = np.abs(w).max(1)
    if fmt == "e4m3":
        byte = np.frexp(amax)[1] - 1 + 127 - 7
    else:
        mant, ex = np.frexp(amax / 6.0)
        byte = np.where(mant > 0.5, ex, ex - 1) + 127
    byte = np.clip(np.where(amax > 0, byte, 1), 1, 254)
    scaled = (w * np.exp2(127.0 - byte)[:, None, :]).reshape(k, n).astype(np.float32)
    by_word = np.ascontiguousarray(scaled.reshape(k // 512, 128, 4, n).transpose(0, 1, 3, 2))
    if fmt == "e4m3":
        words = by_word.astype(ml_dtypes.float8_e4m3fn).view(np.uint8)
    else:
        c = by_word.astype(ml_dtypes.float4_e2m1fn).view(np.uint8) & 0xF
        words = (c[..., 0::2] | (c[..., 1::2] << 4)).reshape(k // 512, 128, 2 * n)
    return np.ascontiguousarray(words), np.ascontiguousarray(byte.astype(np.uint8).reshape(k // 512, 16, n))


def unpack_weight(words, scales, fmt):
    g, _, n = scales.shape
    words = np.ascontiguousarray(words).reshape(g, 128, n, -1)
    if fmt == "e4m3":
        vals = words.view(ml_dtypes.float8_e4m3fn).astype(np.float64)
    else:
        nib = np.empty((g, 128, n, 4), np.uint8)
        nib[..., 0::2] = words & 0xF
        nib[..., 1::2] = words >> 4
        vals = E2M1[nib]
    vals = vals * np.repeat(np.exp2(scales.astype(np.float64) - 127.0), 8, axis=1)[..., None]
    return vals.transpose(0, 1, 3, 2).reshape(g * 512, n)


def planes(y):
    n, m = y.shape
    v = y.astype(np.float32).astype(ml_dtypes.bfloat16).astype(np.float64).reshape(n // 32, 32, m)
    top = np.abs(v).max(1)
    byte = np.clip(np.where(top > 0, np.frexp(top)[1] - 1 + 127 - 7, 1), 1, 254)
    codes = (v * np.exp2(127.0 - byte)[:, None, :]).reshape(n, m).astype(np.float32).astype(ml_dtypes.float8_e4m3fn).view(np.uint8)
    words = codes.reshape(n // 512, 128, 4, m).transpose(0, 1, 3, 2)
    return np.ascontiguousarray(words), np.ascontiguousarray(byte.astype(np.uint8).reshape(n // 512, 16, m))


O, K, M, T = 512, 1536, 1536, 1024


def setup_inputs():
    n = np.random.standard_normal
    s = mx_kscale(K)[:, None]
    x = n((K, T)); x[:O] *= 6.0
    w = n((K, M)) / np.sqrt(K) / s; w[:O] /= 2.0
    p_x4 = pack_weight(x[O:] * s[O:], "e2m1")
    p_w4 = pack_weight(w[O:], "e2m1")
    return {
        "x8": (x[:O] * s[:O]).astype(np.float32),
        "w8": (w[:O]).astype(np.float32),
        "x4_words": p_x4[0],
        "x4_scales": p_x4[1],
        "w4_words": p_w4[0],
        "w4_scales": p_w4[1],
        "r": (n((1536, 1024))).astype(np.float32),
    }


def reference(x8, w8, x4_words, x4_scales, w4_words, w4_scales, r):
    x8_ = mxq(f64(x8), 0, "e4m3")
    w8_ = mxq(f64(w8), 0, "e4m3")
    x4_ = unpack_weight(x4_words, x4_scales, "e2m1")
    w4_ = unpack_weight(w4_words, w4_scales, "e2m1")
    y = w8_.T @ x8_ + w4_.T @ x4_
    out_0 = f64(r) + y
    return (out_0,) + planes(out_0)

@@ -1,0 +1,219 @@
+from contextlib import ExitStack
+
+import concourse.mybir as mybir
+
+O, K4, M, T = 512, 1024, 1536, 1024
+FLOPS = 2 * (O + K4) * M * T
+
+F32 = mybir.dt.float32
+BF16 = mybir.dt.bfloat16
+I32 = mybir.dt.int32
+U32 = mybir.dt.uint32
+U8 = mybir.dt.uint8
+FP8X4 = mybir.dt.float8_e4m3fn_x4
+FP4X4 = mybir.dt.float4_e2m1fn_x4
+ADD = mybir.AluOpType.add
+
+P = 128
+PACK = 4
+SPAN = P * PACK
+N = 512
+GROUPS = M // SPAN
+HALVES = T // N
+PASSES4 = K4 // SPAN
+
+
+def tile_mix_atom_fm_pl_res_kernel(
+    tc, x8, w8, x4_words, x4_scales, w4_words, w4_scales, r, out_0, out_1, out_2
+):
+    nc = tc.nc
+    with ExitStack() as ctx:
+        keep = ctx.enter_context(tc.tile_pool(name="keep", bufs=1))
+        psum = ctx.enter_context(tc.psum_pool(name="psum", bufs=1))
+        ctx.enter_context(tc.manual_schedule())
+
+        def sb(name, shape, dtype):
+            return keep.tile(shape, dtype, name=name, align_bytes=64)
+
+        x8_raw = sb("x8_raw", [P, PACK, T], F32)
+        w8_first = sb("w8_first", [P, PACK, SPAN], F32)
+        w8_rest = sb("w8_rest", [P, PACK, M - SPAN], F32)
+        x4_w = sb("x4_w", [P, PASSES4, 2 * T], U8)
+        x4_s = sb("x4_s", [P, PASSES4, T], U8)
+        w4_w_raw = sb("w4_w_raw", [P, PASSES4, 2 * M], U8)
+        w4_s_raw = sb("w4_s_raw", [P, PASSES4, M], U8)
+        w4_w = [sb(f"w4_w{a}", [P, PASSES4, PACK, 2 * P], U8) for a in range(GROUPS)]
+        w4_s = [sb(f"w4_s{a}", [P, PASSES4, PACK, P], U8) for a in range(GROUPS)]
+        x8_bf = [sb(f"x8_bf{h}", [P, PACK * N], BF16) for h in range(HALVES)]
+        x8_c = [sb(f"x8_c{h}", [P, N], U32) for h in range(HALVES)]
+        x8_s = [sb(f"x8_s{h}", [P, N], U8) for h in range(HALVES)]
+        w8_bf = [sb(f"w8_bf{a}", [P, PACK * SPAN], BF16) for a in range(GROUPS)]
+        w8_c = [sb(f"w8_c{a}", [P, SPAN], U32) for a in range(GROUPS)]
+        w8_s = [sb(f"w8_s{a}", [P, SPAN], U8) for a in range(GROUPS)]
+        res = [sb(f"res{a}", [P, PACK, T], F32) for a in range(GROUPS)]
+        res_bf = [[sb(f"res_bf{a}_{h}", [P, PACK * N], BF16) for h in range(HALVES)] for a in range(GROUPS)]
+        out_c = sb("out_c", [P, GROUPS, T], U32)
+        out_s = sb("out_s", [P, T], U8)
+        banks = {}
+
+        def rows_of(dram, a):
+            return dram[a * SPAN : (a + 1) * SPAN, :].rearrange("(p j) t -> p j t", j=PACK)
+
+        def copy_on(engine, out, in_):
+            if engine == "vector":
+                nc.vector.tensor_copy(out=out, in_=in_)
+            else:
+                nc.scalar.copy(out=out, in_=in_)
+
+        def interleave(engine, dst, src, h):
+            copy_on(
+                engine,
+                dst[:].rearrange("p (c e i) -> p c i e", e=4, i=PACK),
+                src[:, :, h * N : (h + 1) * N].rearrange("p i (c e) -> p c i e", e=4),
+            )
+
+        def deal_w8(engine, a, m0, m1):
+            src = w8_first[:] if a == 0 else w8_rest[:, :, (a - 1) * SPAN : a * SPAN]
+            copy_on(
+                engine,
+                w8_bf[a][:].rearrange("p (j m i) -> p m i j", j=PACK, i=PACK)[:, m0:m1],
+                src.rearrange("p i (m j) -> p m i j", j=PACK)[:, m0:m1],
+            )
+
+        def deal_w4_words(a):
+            for g in range(PASSES4):
+                nc.vector.tensor_copy(
+                    out=w4_w[a][:, g].rearrange("p j (m b) -> p j m b", b=2),
+                    in_=w4_w_raw[:, g, 2 * SPAN * a : 2 * SPAN * (a + 1)].rearrange(
+                        "p (m j b) -> p j m b", j=PACK, b=2
+                    ),
+                )
+
+        def deal_w4_scales(a):
+            nc.vector.tensor_copy(
+                out=w4_s[a][:],
+                in_=w4_s_raw[:, :, SPAN * a : SPAN * (a + 1)].rearrange("p g (m j) -> p g j m", j=PACK),
+            )
+
+        def quantize(codes, scales, values):
+            nc.vector.quantize_mx(out=codes.bitcast(FP8X4), scales=scales, in_=values)
+
+        def quantize_w8(a):
+            quantize(w8_c[a][:], w8_s[a][:], w8_bf[a][:])
+
+        def quantize_res(a, h):
+            cols = slice(h * N, (h + 1) * N)
+            quantize(out_c[:, a, cols], out_s[4 * (a + 1) : P, cols], res_bf[a][h][:])
+
+        def fp4_passes(a, h, j):
+            banks[a, h, j] = psum.tile([P, N], F32, name=f"bank{h}_{j}")
+            for g in range(PASSES4):
+                nc.tensor.matmul_mx(
+                    out=banks[a, h, j][:],
+                    lhsT=w4_w[a][:, g, j, :].bitcast(FP4X4),
+                    lhsT_scale=w4_s[a][:, g, j, :],
+                    rhs=x4_w[:, g, 2 * N * h : 2 * N * (h + 1)].bitcast(FP4X4),
+                    rhs_scale=x4_s[:, g, N * h : N * (h + 1)],
+                    start=(g == 0),
+                    stop=False,
+                )
+
+        def fp8_pass(a, h, j):
+            nc.tensor.matmul_mx(
+                out=banks[a, h, j][:],
+                lhsT=w8_c[a][:, j * P : (j + 1) * P].bitcast(FP8X4),
+                lhsT_scale=w8_s[a][:, j * P : (j + 1) * P],
+                rhs=x8_c[h][:].bitcast(FP8X4),
+                rhs_scale=x8_s[h][:],
+                start=False,
+                stop=True,
+            )
+
+        def add_residual(a, h, j):
+            part = res[a][:, j, h * N : (h + 1) * N]
+            nc.vector.tensor_tensor(out=part, in0=banks[a, h, j][:], in1=part, op=ADD)
+
+        def load_scales(queue, plane, dram):
+            by_row = dram.rearrange("g (q s) n -> s q g n", s=4)
+            for s in range(4):
+                queue.dma_start(out=plane[s:P:32].bitcast(I32), in_=by_row[s].bitcast(I32))
+
+        order = [(h, j) for h in range(HALVES) for j in range(PACK)]
+
+        nc.vector.memset(w4_s_raw[:].rearrange("p g n -> p (g n)").bitcast(I32), 0)
+        nc.vector.memset(x4_s[:].rearrange("p g n -> p (g n)").bitcast(I32), 0)
+        w8_rows = w8.rearrange("(p i) n -> p i n", i=PACK)
+        nc.sync.dma_start(out=w4_w_raw[:].bitcast(I32), in_=w4_words.rearrange("g p b -> p g b").bitcast(I32))
+        nc.sync.dma_start(out=x4_w[:].bitcast(I32), in_=x4_words.rearrange("g p b -> p g b").bitcast(I32))
+        nc.sync.dma_start(out=x8_raw[:], in_=x8.rearrange("(p i) t -> p i t", i=PACK))
+        nc.sync.dma_start(out=w8_first[:], in_=w8_rows[:, :, 0:SPAN])
+        load_scales(nc.scalar, w4_s_raw, w4_scales)
+        load_scales(nc.gpsimd, x4_s, x4_scales)
+        nc.sync.dma_start(out=res[0][:], in_=rows_of(r, 0))
+        nc.sync.dma_start(out=w8_rest[:], in_=w8_rows[:, :, SPAN:M])
+        for a in range(1, GROUPS):
+            nc.sync.dma_start(out=res[a][:], in_=rows_of(r, a))
+
+        deal_w4_words(0)
+        deal_w4_scales(0)
+        for h, j in order:
+            fp4_passes(0, h, j)
+        for a in range(1, GROUPS):
+            deal_w4_words(a)
+            deal_w4_scales(a)
+        interleave("vector", x8_bf[0], x8_raw, 0)
+        interleave("scalar", x8_bf[1], x8_raw, 1)
+        quantize(x8_c[0][:], x8_s[0][:], x8_bf[0][:])
+        deal_w8("vector", 0, 0, P // 2)
+        deal_w8("scalar", 0, P // 2, P)
+        quantize(x8_c[1][:], x8_s[1][:], x8_bf[1][:])
+        quantize_w8(0)
+        for h, j in order:
+            fp8_pass(0, h, j)
+
+        for h, j in order:
+            add_residual(0, h, j)
+            fp4_passes(1, h, j)
+            if j == PACK - 1:
+                interleave("scalar", res_bf[0][h], res[0], h)
+        nc.sync.dma_start(out=rows_of(out_0, 0), in_=res[0][:])
+        deal_w8("vector", 1, 0, P)
+        deal_w8("scalar", 2, 0, P)
+        quantize_res(0, 0)
+        quantize_w8(1)
+        for h, j in order:
+            fp8_pass(1, h, j)
+        quantize_res(0, 1)
+
+        for h, j in order:
+            add_residual(1, h, j)
+            if (h, j) == (0, 1):
+                quantize_w8(2)
+            fp4_passes(2, h, j)
+            if (h, j) == (0, 1):
+                fp8_pass(2, 0, 0)
+            if (h, j) != (0, 0):
+                fp8_pass(2, h, j)
+            if j == PACK - 1:
+                interleave("scalar", res_bf[1][h], res[1], h)
+        nc.sync.dma_start(out=rows_of(out_0, 1), in_=res[1][:])
+        quantize_res(1, 0)
+
+        for h, j in order:
+            add_residual(2, h, j)
+            if (h, j) == (0, PACK - 1):
+                interleave("scalar", res_bf[2][0], res[2], 0)
+            if (h, j) == (1, 0):
+                quantize_res(1, 1)
+        nc.sync.dma_start(out=rows_of(out_0, 2), in_=res[2][:])
+        interleave("vector", res_bf[2][1], res[2], 1)
+        quantize_res(2, 0)
+        quantize_res(2, 1)
+        nc.sync.dma_start(
+            out=out_1.rearrange("a p t b -> p a (t b)").bitcast(I32), in_=out_c[:].bitcast(I32)
+        )
+        for q in range(4):
+            nc.gpsimd.dma_start(
+                out=out_2[:, 4 * q : 4 * q + 4, :].bitcast(I32),
+                in_=out_s[32 * q + 4 : 32 * q + 16, :].bitcast(I32),
+            )

@@ -36,8 +36,7 @@ def tile_mix_atom_fm_pl_res_kernel(
             return keep.tile(shape, dtype, name=name, align_bytes=64)
 
         x8_raw = sb("x8_raw", [P, PACK, T], F32)
-        w8_first = sb("w8_first", [P, PACK, SPAN], F32)
-        w8_rest = sb("w8_rest", [P, PACK, M - SPAN], F32)
+        w8_raw = [sb(f"w8_raw{a}", [P, PACK, SPAN], F32) for a in range(GROUPS)]
         x4_w = sb("x4_w", [P, PASSES4, 2 * T], U8)
         x4_s = sb("x4_s", [P, PASSES4, T], U8)
         w4_w_raw = sb("w4_w_raw", [P, PASSES4, 2 * M], U8)
@@ -53,7 +52,7 @@ def tile_mix_atom_fm_pl_res_kernel(
         res = [sb(f"res{a}", [P, PACK, T], F32) for a in range(GROUPS)]
         res_bf = [[sb(f"res_bf{a}_{h}", [P, PACK * N], BF16) for h in range(HALVES)] for a in range(GROUPS)]
         out_c = sb("out_c", [P, GROUPS, T], U32)
-        out_s = sb("out_s", [P, T], U8)
+        out_s = [sb("out_s_early", [P, T], U8), sb("out_s_last", [P, T], U8)]
         banks = {}
 
         def rows_of(dram, a):
@@ -73,11 +72,11 @@ def tile_mix_atom_fm_pl_res_kernel(
             )
 
         def deal_w8(engine, a, m0, m1):
-            src = w8_first[:] if a == 0 else w8_rest[:, :, (a - 1) * SPAN : a * SPAN]
+            src = w8_raw[a][:]
             copy_on(
                 engine,
-                w8_bf[a][:].rearrange("p (j m i) -> p m i j", j=PACK, i=PACK)[:, m0:m1],
-                src.rearrange("p i (m j) -> p m i j", j=PACK)[:, m0:m1],
+                w8_bf[a][:].rearrange("p (j m i) -> p m j i", j=PACK, i=PACK)[:, :, m0:m1],
+                src.rearrange("p i (m j) -> p m j i", j=PACK)[:, :, m0:m1],
             )
 
         def deal_w4_words(a):
@@ -103,7 +102,7 @@ def tile_mix_atom_fm_pl_res_kernel(
 
         def quantize_res(a, h):
             cols = slice(h * N, (h + 1) * N)
-            quantize(out_c[:, a, cols], out_s[4 * (a + 1) : P, cols], res_bf[a][h][:])
+            quantize(out_c[:, a, cols], out_s[a // 2][4 * (a + 1) : P, cols], res_bf[a][h][:])
 
         def fp4_passes(a, h, j):
             banks[a, h, j] = psum.tile([P, N], F32, name=f"bank{h}_{j}")
@@ -138,82 +137,82 @@ def tile_mix_atom_fm_pl_res_kernel(
             for s in range(4):
                 queue.dma_start(out=plane[s:P:32].bitcast(I32), in_=by_row[s].bitcast(I32))
 
-        order = [(h, j) for h in range(HALVES) for j in range(PACK)]
+        order = [(h, j) for j in range(PACK) for h in range(HALVES)]
 
         nc.vector.memset(w4_s_raw[:].rearrange("p g n -> p (g n)").bitcast(I32), 0)
         nc.vector.memset(x4_s[:].rearrange("p g n -> p (g n)").bitcast(I32), 0)
         w8_rows = w8.rearrange("(p i) n -> p i n", i=PACK)
         nc.sync.dma_start(out=w4_w_raw[:].bitcast(I32), in_=w4_words.rearrange("g p b -> p g b").bitcast(I32))
-        nc.sync.dma_start(out=x4_w[:].bitcast(I32), in_=x4_words.rearrange("g p b -> p g b").bitcast(I32))
+        load_scales(nc.sync, w4_s_raw, w4_scales)
         nc.sync.dma_start(out=x8_raw[:], in_=x8.rearrange("(p i) t -> p i t", i=PACK))
-        nc.sync.dma_start(out=w8_first[:], in_=w8_rows[:, :, 0:SPAN])
-        load_scales(nc.scalar, w4_s_raw, w4_scales)
-        load_scales(nc.gpsimd, x4_s, x4_scales)
-        nc.sync.dma_start(out=res[0][:], in_=rows_of(r, 0))
-        nc.sync.dma_start(out=w8_rest[:], in_=w8_rows[:, :, SPAN:M])
+        nc.sync.dma_start(out=x4_w[:].bitcast(I32), in_=x4_words.rearrange("g p b -> p g b").bitcast(I32))
+        load_scales(nc.sync, x4_s, x4_scales)
+        for a in range(2):
+            nc.sync.dma_start(out=w8_raw[a][:], in_=w8_rows[:, :, a * SPAN : (a + 1) * SPAN])
+        for j in range(0, PACK, 2):
+            nc.sync.dma_start(out=res[0][:, j : j + 2, :], in_=rows_of(r, 0)[:, j : j + 2, :])
+        nc.sync.dma_start(out=w8_raw[2][:], in_=w8_rows[:, :, 2 * SPAN : 3 * SPAN])
         for a in range(1, GROUPS):
             nc.sync.dma_start(out=res[a][:], in_=rows_of(r, a))
+
+        def store_codes(a):
+            nc.sync.dma_start(
+                out=out_1[a].rearrange("p t b -> p (t b)").bitcast(I32), in_=out_c[:, a, :].bitcast(I32)
+            )
+
+        def store_scales(a0, a1):
+            for q in range(4):
+                nc.sync.dma_start(
+                    out=out_2[a0:a1, 4 * q : 4 * q + 4, :].bitcast(I32),
+                    in_=out_s[a0 // 2][32 * q + 4 * (a0 + 1) : 32 * q + 4 * (a1 + 1), :].bitcast(I32),
+                )
 
         deal_w4_words(0)
         deal_w4_scales(0)
         for h, j in order:
             fp4_passes(0, h, j)
-        for a in range(1, GROUPS):
-            deal_w4_words(a)
-            deal_w4_scales(a)
+        deal_w4_words(1)
+        deal_w4_scales(1)
         interleave("vector", x8_bf[0], x8_raw, 0)
         interleave("scalar", x8_bf[1], x8_raw, 1)
         quantize(x8_c[0][:], x8_s[0][:], x8_bf[0][:])
-        deal_w8("vector", 0, 0, P // 2)
-        deal_w8("scalar", 0, P // 2, P)
+        deal_w8("vector", 0, 0, 2)
+        deal_w8("scalar", 0, 2, 4)
         quantize(x8_c[1][:], x8_s[1][:], x8_bf[1][:])
         quantize_w8(0)
         for h, j in order:
             fp8_pass(0, h, j)
+        deal_w4_words(2)
+        deal_w4_scales(2)
+        deal_w8("scalar", 1, 0, 4)
+        deal_w8("scalar", 2, 0, 4)
 
-        for h, j in order:
-            add_residual(0, h, j)
-            fp4_passes(1, h, j)
-            if j == PACK - 1:
-                interleave("scalar", res_bf[0][h], res[0], h)
-        nc.sync.dma_start(out=rows_of(out_0, 0), in_=res[0][:])
-        deal_w8("vector", 1, 0, P)
-        deal_w8("scalar", 2, 0, P)
-        quantize_res(0, 0)
-        quantize_w8(1)
-        for h, j in order:
-            fp8_pass(1, h, j)
-        quantize_res(0, 1)
-
-        for h, j in order:
-            add_residual(1, h, j)
-            if (h, j) == (0, 1):
+        for a in range(GROUPS):
+            if a == 1:
                 quantize_w8(2)
-            fp4_passes(2, h, j)
-            if (h, j) == (0, 1):
-                fp8_pass(2, 0, 0)
-            if (h, j) != (0, 0):
-                fp8_pass(2, h, j)
-            if j == PACK - 1:
-                interleave("scalar", res_bf[1][h], res[1], h)
-        nc.sync.dma_start(out=rows_of(out_0, 1), in_=res[1][:])
-        quantize_res(1, 0)
-
-        for h, j in order:
-            add_residual(2, h, j)
-            if (h, j) == (0, PACK - 1):
-                interleave("scalar", res_bf[2][0], res[2], 0)
-            if (h, j) == (1, 0):
-                quantize_res(1, 1)
-        nc.sync.dma_start(out=rows_of(out_0, 2), in_=res[2][:])
+            if a == 2:
+                quantize_res(0, 0)
+                quantize_res(0, 1)
+                store_codes(0)
+            for h, j in order:
+                add_residual(a, h, j)
+                if (a, h, j) == (0, 0, 0):
+                    quantize_w8(1)
+                if a + 1 < GROUPS:
+                    fp4_passes(a + 1, h, j)
+                    fp8_pass(a + 1, h, j)
+                if a == GROUPS - 1 and h == HALVES - 1 and j % 2 == 1:
+                    nc.sync.dma_start(out=rows_of(out_0, a)[:, j - 1 : j + 1, :], in_=res[a][:, j - 1 : j + 1, :])
+            interleave("scalar", res_bf[a][0], res[a], 0)
+            if a < GROUPS - 1:
+                interleave("scalar", res_bf[a][1], res[a], 1)
+                nc.sync.dma_start(out=rows_of(out_0, a), in_=res[a][:])
         interleave("vector", res_bf[2][1], res[2], 1)
-        quantize_res(2, 0)
+        quantize_res(1, 0)
+        quantize_res(1, 1)
+        store_scales(0, 2)
+        store_codes(1)
         quantize_res(2, 1)
-        nc.sync.dma_start(
-            out=out_1.rearrange("a p t b -> p a (t b)").bitcast(I32), in_=out_c[:].bitcast(I32)
-        )
-        for q in range(4):
-            nc.gpsimd.dma_start(
-                out=out_2[:, 4 * q : 4 * q + 4, :].bitcast(I32),
-                in_=out_s[32 * q + 4 : 32 * q + 16, :].bitcast(I32),
-            )
+        quantize_res(2, 0)
+        store_scales(2, 3)
+        store_codes(2)

@@ -52,7 +52,7 @@ def tile_mix_atom_fm_pl_res_kernel(
         res = [sb(f"res{a}", [P, PACK, T], F32) for a in range(GROUPS)]
         res_bf = [[sb(f"res_bf{a}_{h}", [P, PACK * N], BF16) for h in range(HALVES)] for a in range(GROUPS)]
         out_c = sb("out_c", [P, GROUPS, T], U32)
-        out_s = [sb("out_s_early", [P, T], U8), sb("out_s_last", [P, T], U8)]
+        out_s = sb("out_s", [P, T], U8)
         banks = {}
 
         def rows_of(dram, a):
@@ -102,7 +102,7 @@ def tile_mix_atom_fm_pl_res_kernel(
 
         def quantize_res(a, h):
             cols = slice(h * N, (h + 1) * N)
-            quantize(out_c[:, a, cols], out_s[a // 2][4 * (a + 1) : P, cols], res_bf[a][h][:])
+            quantize(out_c[:, a, cols], out_s[4 * (a + 1) : P, cols], res_bf[a][h][:])
 
         def fp4_passes(a, h, j):
             banks[a, h, j] = psum.tile([P, N], F32, name=f"bank{h}_{j}")
@@ -139,14 +139,14 @@ def tile_mix_atom_fm_pl_res_kernel(
 
         order = [(h, j) for j in range(PACK) for h in range(HALVES)]
 
-        nc.vector.memset(w4_s_raw[:].rearrange("p g n -> p (g n)").bitcast(I32), 0)
         nc.vector.memset(x4_s[:].rearrange("p g n -> p (g n)").bitcast(I32), 0)
+        nc.vector.memset(w4_s_raw[:].rearrange("p g n -> p (g n)").bitcast(I32), 0)
+        load_scales(nc.gpsimd, x4_s, x4_scales)
         w8_rows = w8.rearrange("(p i) n -> p i n", i=PACK)
         nc.sync.dma_start(out=w4_w_raw[:].bitcast(I32), in_=w4_words.rearrange("g p b -> p g b").bitcast(I32))
         load_scales(nc.sync, w4_s_raw, w4_scales)
         nc.sync.dma_start(out=x8_raw[:], in_=x8.rearrange("(p i) t -> p i t", i=PACK))
         nc.sync.dma_start(out=x4_w[:].bitcast(I32), in_=x4_words.rearrange("g p b -> p g b").bitcast(I32))
-        load_scales(nc.sync, x4_s, x4_scales)
         for a in range(2):
             nc.sync.dma_start(out=w8_raw[a][:], in_=w8_rows[:, :, a * SPAN : (a + 1) * SPAN])
         for j in range(0, PACK, 2):
@@ -155,16 +155,17 @@ def tile_mix_atom_fm_pl_res_kernel(
         for a in range(1, GROUPS):
             nc.sync.dma_start(out=res[a][:], in_=rows_of(r, a))
 
-        def store_codes(a):
+        def store_codes(a0, a1):
             nc.sync.dma_start(
-                out=out_1[a].rearrange("p t b -> p (t b)").bitcast(I32), in_=out_c[:, a, :].bitcast(I32)
+                out=out_1[a0:a1].rearrange("a p t b -> p a (t b)").bitcast(I32),
+                in_=out_c[:, a0:a1, :].bitcast(I32),
             )
 
-        def store_scales(a0, a1):
+        def store_scales():
             for q in range(4):
-                nc.sync.dma_start(
-                    out=out_2[a0:a1, 4 * q : 4 * q + 4, :].bitcast(I32),
-                    in_=out_s[a0 // 2][32 * q + 4 * (a0 + 1) : 32 * q + 4 * (a1 + 1), :].bitcast(I32),
+                nc.gpsimd.dma_start(
+                    out=out_2[:, 4 * q : 4 * q + 4, :].bitcast(I32),
+                    in_=out_s[32 * q + 4 : 32 * q + 16, :].bitcast(I32),
                 )
 
         deal_w4_words(0)
@@ -193,7 +194,7 @@ def tile_mix_atom_fm_pl_res_kernel(
             if a == 2:
                 quantize_res(0, 0)
                 quantize_res(0, 1)
-                store_codes(0)
+                store_codes(0, 1)
             for h, j in order:
                 add_residual(a, h, j)
                 if (a, h, j) == (0, 0, 0):
@@ -201,18 +202,14 @@ def tile_mix_atom_fm_pl_res_kernel(
                 if a + 1 < GROUPS:
                     fp4_passes(a + 1, h, j)
                     fp8_pass(a + 1, h, j)
-                if a == GROUPS - 1 and h == HALVES - 1 and j % 2 == 1:
-                    nc.sync.dma_start(out=rows_of(out_0, a)[:, j - 1 : j + 1, :], in_=res[a][:, j - 1 : j + 1, :])
             interleave("scalar", res_bf[a][0], res[a], 0)
             if a < GROUPS - 1:
                 interleave("scalar", res_bf[a][1], res[a], 1)
-                nc.sync.dma_start(out=rows_of(out_0, a), in_=res[a][:])
+            nc.sync.dma_start(out=rows_of(out_0, a), in_=res[a][:])
         interleave("vector", res_bf[2][1], res[2], 1)
         quantize_res(1, 0)
         quantize_res(1, 1)
-        store_scales(0, 2)
-        store_codes(1)
         quantize_res(2, 1)
         quantize_res(2, 0)
-        store_scales(2, 3)
-        store_codes(2)
+        store_scales()
+        store_codes(1, 3)

@@ -9,6 +9,7 @@ F32 = mybir.dt.float32
 BF16 = mybir.dt.bfloat16
 I32 = mybir.dt.int32
 U32 = mybir.dt.uint32
+U16 = mybir.dt.uint16
 U8 = mybir.dt.uint8
 FP8X4 = mybir.dt.float8_e4m3fn_x4
 FP4X4 = mybir.dt.float4_e2m1fn_x4
@@ -36,7 +37,7 @@ def tile_mix_atom_fm_pl_res_kernel(
             return keep.tile(shape, dtype, name=name, align_bytes=64)
 
         x8_raw = sb("x8_raw", [P, PACK, T], F32)
-        w8_raw = [sb(f"w8_raw{a}", [P, PACK, SPAN], F32) for a in range(GROUPS)]
+        w8_raw = sb("w8_raw", [P, PACK, M], F32)
         x4_w = sb("x4_w", [P, PASSES4, 2 * T], U8)
         x4_s = sb("x4_s", [P, PASSES4, T], U8)
         w4_w_raw = sb("w4_w_raw", [P, PASSES4, 2 * M], U8)
@@ -51,8 +52,10 @@ def tile_mix_atom_fm_pl_res_kernel(
         w8_s = [sb(f"w8_s{a}", [P, SPAN], U8) for a in range(GROUPS)]
         res = [sb(f"res{a}", [P, PACK, T], F32) for a in range(GROUPS)]
         res_bf = [[sb(f"res_bf{a}_{h}", [P, PACK * N], BF16) for h in range(HALVES)] for a in range(GROUPS)]
-        out_c = sb("out_c", [P, GROUPS, T], U32)
-        out_s = sb("out_s", [P, T], U8)
+        out_c = [sb(f"out_c{a}", [P, T], U32) for a in range(GROUPS)]
+        early_s = sb("early_s", [P, T], U8)
+        last_s = sb("last_s", [P, T], U8)
+        out_s = [early_s, early_s, last_s]
         banks = {}
 
         def rows_of(dram, a):
@@ -71,22 +74,18 @@ def tile_mix_atom_fm_pl_res_kernel(
                 src[:, :, h * N : (h + 1) * N].rearrange("p i (c e) -> p c i e", e=4),
             )
 
-        def deal_w8(engine, a, m0, m1):
-            src = w8_raw[a][:]
+        def deal_w8(engine, a):
             copy_on(
                 engine,
-                w8_bf[a][:].rearrange("p (j m i) -> p m j i", j=PACK, i=PACK)[:, :, m0:m1],
-                src.rearrange("p i (m j) -> p m j i", j=PACK)[:, :, m0:m1],
+                w8_bf[a][:].rearrange("p (j m i) -> p m j i", j=PACK, i=PACK),
+                w8_raw[:, :, a * SPAN : (a + 1) * SPAN].rearrange("p i (m j) -> p m j i", j=PACK),
             )
 
         def deal_w4_words(a):
-            for g in range(PASSES4):
-                nc.vector.tensor_copy(
-                    out=w4_w[a][:, g].rearrange("p j (m b) -> p j m b", b=2),
-                    in_=w4_w_raw[:, g, 2 * SPAN * a : 2 * SPAN * (a + 1)].rearrange(
-                        "p (m j b) -> p j m b", j=PACK, b=2
-                    ),
-                )
+            nc.vector.tensor_copy(
+                out=w4_w[a][:].bitcast(U16),
+                in_=w4_w_raw[:].bitcast(U16)[:, :, SPAN * a : SPAN * (a + 1)].rearrange("p g (m j) -> p g j m", j=PACK),
+            )
 
         def deal_w4_scales(a):
             nc.vector.tensor_copy(
@@ -100,9 +99,12 @@ def tile_mix_atom_fm_pl_res_kernel(
         def quantize_w8(a):
             quantize(w8_c[a][:], w8_s[a][:], w8_bf[a][:])
 
+        def quantize_x8(h):
+            quantize(x8_c[h][:], x8_s[h][:], x8_bf[h][:])
+
         def quantize_res(a, h):
             cols = slice(h * N, (h + 1) * N)
-            quantize(out_c[:, a, cols], out_s[4 * (a + 1) : P, cols], res_bf[a][h][:])
+            quantize(out_c[a][:, cols], out_s[a][4 * (a + 1) : P, cols], res_bf[a][h][:])
 
         def fp4_passes(a, h, j):
             banks[a, h, j] = psum.tile([P, N], F32, name=f"bank{h}_{j}")
@@ -137,79 +139,78 @@ def tile_mix_atom_fm_pl_res_kernel(
             for s in range(4):
                 queue.dma_start(out=plane[s:P:32].bitcast(I32), in_=by_row[s].bitcast(I32))
 
-        order = [(h, j) for j in range(PACK) for h in range(HALVES)]
-
-        nc.vector.memset(x4_s[:].rearrange("p g n -> p (g n)").bitcast(I32), 0)
-        nc.vector.memset(w4_s_raw[:].rearrange("p g n -> p (g n)").bitcast(I32), 0)
-        load_scales(nc.gpsimd, x4_s, x4_scales)
-        w8_rows = w8.rearrange("(p i) n -> p i n", i=PACK)
-        nc.sync.dma_start(out=w4_w_raw[:].bitcast(I32), in_=w4_words.rearrange("g p b -> p g b").bitcast(I32))
-        load_scales(nc.sync, w4_s_raw, w4_scales)
-        nc.sync.dma_start(out=x8_raw[:], in_=x8.rearrange("(p i) t -> p i t", i=PACK))
-        nc.sync.dma_start(out=x4_w[:].bitcast(I32), in_=x4_words.rearrange("g p b -> p g b").bitcast(I32))
-        for a in range(2):
-            nc.sync.dma_start(out=w8_raw[a][:], in_=w8_rows[:, :, a * SPAN : (a + 1) * SPAN])
-        for j in range(0, PACK, 2):
-            nc.sync.dma_start(out=res[0][:, j : j + 2, :], in_=rows_of(r, 0)[:, j : j + 2, :])
-        nc.sync.dma_start(out=w8_raw[2][:], in_=w8_rows[:, :, 2 * SPAN : 3 * SPAN])
-        for a in range(1, GROUPS):
-            nc.sync.dma_start(out=res[a][:], in_=rows_of(r, a))
-
-        def store_codes(a0, a1):
+        def store_codes(a):
             nc.sync.dma_start(
-                out=out_1[a0:a1].rearrange("a p t b -> p a (t b)").bitcast(I32),
-                in_=out_c[:, a0:a1, :].bitcast(I32),
+                out=out_1[a].rearrange("p t b -> p (t b)").bitcast(I32),
+                in_=out_c[a][:].bitcast(I32),
             )
 
-        def store_scales():
+        def store_early_scales():
             for q in range(4):
                 nc.gpsimd.dma_start(
-                    out=out_2[:, 4 * q : 4 * q + 4, :].bitcast(I32),
-                    in_=out_s[32 * q + 4 : 32 * q + 16, :].bitcast(I32),
+                    out=out_2[0:2, 4 * q : 4 * q + 4, :].bitcast(I32),
+                    in_=early_s[32 * q + 4 : 32 * q + 12, :].bitcast(I32),
                 )
 
-        deal_w4_words(0)
-        deal_w4_scales(0)
-        for h, j in order:
-            fp4_passes(0, h, j)
-        deal_w4_words(1)
-        deal_w4_scales(1)
-        interleave("vector", x8_bf[0], x8_raw, 0)
-        interleave("scalar", x8_bf[1], x8_raw, 1)
-        quantize(x8_c[0][:], x8_s[0][:], x8_bf[0][:])
-        deal_w8("vector", 0, 0, 2)
-        deal_w8("scalar", 0, 2, 4)
-        quantize(x8_c[1][:], x8_s[1][:], x8_bf[1][:])
-        quantize_w8(0)
-        for h, j in order:
-            fp8_pass(0, h, j)
-        deal_w4_words(2)
-        deal_w4_scales(2)
-        deal_w8("scalar", 1, 0, 4)
-        deal_w8("scalar", 2, 0, 4)
+        def store_last_scales():
+            by_row = out_2[GROUPS - 1].rearrange("(q s) n -> s q n", s=4)
+            for s in range(4):
+                nc.sync.dma_start(out=by_row[s].bitcast(I32), in_=last_s[12 + s : P : 32].bitcast(I32))
+
+        def store_res(a):
+            nc.sync.dma_start(out=rows_of(out_0, a), in_=res[a][:])
+
+        order = [(h, j) for j in range(PACK) for h in range(HALVES)]
+
+        nc.vector.memset(w4_s_raw[:].rearrange("p g n -> p (g n)").bitcast(I32), 0)
+        nc.vector.memset(x4_s[:].rearrange("p g n -> p (g n)").bitcast(I32), 0)
+        load_scales(nc.gpsimd, w4_s_raw, w4_scales)
+        load_scales(nc.gpsimd, x4_s, x4_scales)
+        nc.sync.dma_start(out=w4_w_raw[:].bitcast(I32), in_=w4_words.rearrange("g p b -> p g b").bitcast(I32))
+        nc.sync.dma_start(out=x4_w[:].bitcast(I32), in_=x4_words.rearrange("g p b -> p g b").bitcast(I32))
+        nc.sync.dma_start(out=w8_raw[:], in_=w8.rearrange("(p i) n -> p i n", i=PACK))
+        nc.sync.dma_start(out=x8_raw[:], in_=x8.rearrange("(p i) t -> p i t", i=PACK))
+        for a in range(GROUPS):
+            nc.sync.dma_start(out=res[a][:], in_=rows_of(r, a))
 
         for a in range(GROUPS):
-            if a == 1:
-                quantize_w8(2)
-            if a == 2:
-                quantize_res(0, 0)
-                quantize_res(0, 1)
-                store_codes(0, 1)
-            for h, j in order:
+            deal_w4_scales(a)
+            deal_w4_words(a)
+        for h, j in order:
+            fp4_passes(0, h, j)
+        deal_w8("vector", 0)
+        deal_w8("scalar", 1)
+        deal_w8("scalar", 2)
+        quantize_w8(0)
+        quantize_w8(1)
+        interleave("vector", x8_bf[0], x8_raw, 0)
+        interleave("scalar", x8_bf[1], x8_raw, 1)
+        quantize_w8(2)
+        quantize_x8(0)
+        quantize_x8(1)
+        for h in range(HALVES):
+            for j in range(PACK):
+                fp8_pass(0, h, j)
+
+        for a in range(GROUPS):
+            for step, (h, j) in enumerate(order):
                 add_residual(a, h, j)
-                if (a, h, j) == (0, 0, 0):
-                    quantize_w8(1)
                 if a + 1 < GROUPS:
                     fp4_passes(a + 1, h, j)
                     fp8_pass(a + 1, h, j)
+                if a == 2 and step in (3, 6):
+                    quantize_res(1, step // 4)
+            if a == 1:
+                quantize_res(0, 0)
+                quantize_res(0, 1)
+                store_codes(0)
+            if a == 2:
+                store_codes(1)
+                store_early_scales()
+            store_res(a)
             interleave("scalar", res_bf[a][0], res[a], 0)
-            if a < GROUPS - 1:
-                interleave("scalar", res_bf[a][1], res[a], 1)
-            nc.sync.dma_start(out=rows_of(out_0, a), in_=res[a][:])
-        interleave("vector", res_bf[2][1], res[2], 1)
-        quantize_res(1, 0)
-        quantize_res(1, 1)
+            interleave("scalar" if a < GROUPS - 1 else "vector", res_bf[a][1], res[a], 1)
         quantize_res(2, 1)
         quantize_res(2, 0)
-        store_scales()
-        store_codes(1, 3)
+        store_last_scales()
+        store_codes(2)

@@ -53,9 +53,9 @@ def tile_mix_atom_fm_pl_res_kernel(
         res = [sb(f"res{a}", [P, PACK, T], F32) for a in range(GROUPS)]
         res_bf = [[sb(f"res_bf{a}_{h}", [P, PACK * N], BF16) for h in range(HALVES)] for a in range(GROUPS)]
         out_c = [sb(f"out_c{a}", [P, T], U32) for a in range(GROUPS)]
-        early_s = sb("early_s", [P, T], U8)
-        last_s = sb("last_s", [P, T], U8)
-        out_s = [early_s, early_s, last_s]
+        first_s = sb("first_s", [P, T], U8)
+        late_s = sb("late_s", [P, T], U8)
+        out_s = [first_s, late_s, late_s]
         banks = {}
 
         def rows_of(dram, a):
@@ -74,11 +74,11 @@ def tile_mix_atom_fm_pl_res_kernel(
                 src[:, :, h * N : (h + 1) * N].rearrange("p i (c e) -> p c i e", e=4),
             )
 
-        def deal_w8(engine, a):
+        def deal_w8(engine, a, j0=0, j1=PACK):
             copy_on(
                 engine,
-                w8_bf[a][:].rearrange("p (j m i) -> p m j i", j=PACK, i=PACK),
-                w8_raw[:, :, a * SPAN : (a + 1) * SPAN].rearrange("p i (m j) -> p m j i", j=PACK),
+                w8_bf[a][:].rearrange("p (j m i) -> p m j i", j=PACK, i=PACK)[:, :, j0:j1],
+                w8_raw[:, :, a * SPAN : (a + 1) * SPAN].rearrange("p i (m j) -> p m j i", j=PACK)[:, :, j0:j1],
             )
 
         def deal_w4_words(a):
@@ -145,72 +145,77 @@ def tile_mix_atom_fm_pl_res_kernel(
                 in_=out_c[a][:].bitcast(I32),
             )
 
-        def store_early_scales():
-            for q in range(4):
-                nc.gpsimd.dma_start(
-                    out=out_2[0:2, 4 * q : 4 * q + 4, :].bitcast(I32),
-                    in_=early_s[32 * q + 4 : 32 * q + 12, :].bitcast(I32),
-                )
-
-        def store_last_scales():
-            by_row = out_2[GROUPS - 1].rearrange("(q s) n -> s q n", s=4)
+        def store_first_scales():
+            by_row = out_2[0].rearrange("(q s) n -> s q n", s=4)
             for s in range(4):
-                nc.sync.dma_start(out=by_row[s].bitcast(I32), in_=last_s[12 + s : P : 32].bitcast(I32))
+                nc.gpsimd.dma_start(out=by_row[s].bitcast(I32), in_=first_s[4 + s : P : 32].bitcast(I32))
+
+        def store_late_scales():
+            for q in range(4):
+                nc.sync.dma_start(
+                    out=out_2[1:3, 4 * q : 4 * q + 4, :].bitcast(I32),
+                    in_=late_s[32 * q + 8 : 32 * q + 16, :].bitcast(I32),
+                )
 
         def store_res(a):
             nc.sync.dma_start(out=rows_of(out_0, a), in_=res[a][:])
 
         order = [(h, j) for j in range(PACK) for h in range(HALVES)]
 
-        nc.vector.memset(w4_s_raw[:].rearrange("p g n -> p (g n)").bitcast(I32), 0)
         nc.vector.memset(x4_s[:].rearrange("p g n -> p (g n)").bitcast(I32), 0)
-        load_scales(nc.gpsimd, w4_s_raw, w4_scales)
+        nc.vector.memset(w4_s_raw[:].rearrange("p g n -> p (g n)").bitcast(I32), 0)
         load_scales(nc.gpsimd, x4_s, x4_scales)
         nc.sync.dma_start(out=w4_w_raw[:].bitcast(I32), in_=w4_words.rearrange("g p b -> p g b").bitcast(I32))
+        load_scales(nc.sync, w4_s_raw, w4_scales)
+        nc.sync.dma_start(out=x8_raw[:], in_=x8.rearrange("(p i) t -> p i t", i=PACK))
         nc.sync.dma_start(out=x4_w[:].bitcast(I32), in_=x4_words.rearrange("g p b -> p g b").bitcast(I32))
         nc.sync.dma_start(out=w8_raw[:], in_=w8.rearrange("(p i) n -> p i n", i=PACK))
-        nc.sync.dma_start(out=x8_raw[:], in_=x8.rearrange("(p i) t -> p i t", i=PACK))
-        for a in range(GROUPS):
+        for j in range(0, PACK, 2):
+            nc.sync.dma_start(out=res[0][:, j : j + 2, :], in_=rows_of(r, 0)[:, j : j + 2, :])
+        for a in range(1, GROUPS):
             nc.sync.dma_start(out=res[a][:], in_=rows_of(r, a))
 
         for a in range(GROUPS):
-            deal_w4_scales(a)
             deal_w4_words(a)
+            deal_w4_scales(a)
         for h, j in order:
             fp4_passes(0, h, j)
-        deal_w8("vector", 0)
+        interleave("vector", x8_bf[0], x8_raw, 0)
+        interleave("scalar", x8_bf[1], x8_raw, 1)
+        quantize_x8(0)
+        quantize_x8(1)
+        deal_w8("vector", 0, 0, 3)
+        deal_w8("scalar", 0, 3, 4)
         deal_w8("scalar", 1)
         deal_w8("scalar", 2)
         quantize_w8(0)
-        quantize_w8(1)
-        interleave("vector", x8_bf[0], x8_raw, 0)
-        interleave("scalar", x8_bf[1], x8_raw, 1)
-        quantize_w8(2)
-        quantize_x8(0)
-        quantize_x8(1)
-        for h in range(HALVES):
-            for j in range(PACK):
-                fp8_pass(0, h, j)
+        for h, j in order:
+            fp8_pass(0, h, j)
 
+        late = {(0, 1): lambda: quantize_w8(1), (0, 7): lambda: quantize_w8(2),
+                (1, 7): lambda: quantize_res(0, 0), (2, 2): lambda: quantize_res(0, 1), (2, 6): lambda: quantize_res(1, 0)}
+        pending = []
         for a in range(GROUPS):
             for step, (h, j) in enumerate(order):
                 add_residual(a, h, j)
+                if (a, step) in late:
+                    late[a, step]()
                 if a + 1 < GROUPS:
-                    fp4_passes(a + 1, h, j)
-                    fp8_pass(a + 1, h, j)
-                if a == 2 and step in (3, 6):
-                    quantize_res(1, step // 4)
-            if a == 1:
-                quantize_res(0, 0)
-                quantize_res(0, 1)
-                store_codes(0)
-            if a == 2:
-                store_codes(1)
-                store_early_scales()
+                    pending.append((a + 1, h, j))
+                    if (a, step) != (0, 0):
+                        for item in pending:
+                            fp4_passes(*item)
+                            fp8_pass(*item)
+                        pending.clear()
+                if (a, step) == (2, 2):
+                    store_codes(0)
+                    store_first_scales()
             store_res(a)
             interleave("scalar", res_bf[a][0], res[a], 0)
             interleave("scalar" if a < GROUPS - 1 else "vector", res_bf[a][1], res[a], 1)
+        quantize_res(1, 1)
+        store_codes(1)
         quantize_res(2, 1)
         quantize_res(2, 0)
-        store_last_scales()
+        store_late_scales()
         store_codes(2)

@@ -192,27 +192,41 @@ def tile_mix_atom_fm_pl_res_kernel(
         for h, j in order:
             fp8_pass(0, h, j)
 
-        late = {(0, 1): lambda: quantize_w8(1), (0, 7): lambda: quantize_w8(2),
-                (1, 7): lambda: quantize_res(0, 0), (2, 2): lambda: quantize_res(0, 1), (2, 6): lambda: quantize_res(1, 0)}
-        pending = []
-        for a in range(GROUPS):
-            for step, (h, j) in enumerate(order):
+        def adds(a, first, last):
+            for h, j in order[first:last]:
                 add_residual(a, h, j)
-                if (a, step) in late:
-                    late[a, step]()
-                if a + 1 < GROUPS:
-                    pending.append((a + 1, h, j))
-                    if (a, step) != (0, 0):
-                        for item in pending:
-                            fp4_passes(*item)
-                            fp8_pass(*item)
-                        pending.clear()
-                if (a, step) == (2, 2):
-                    store_codes(0)
-                    store_first_scales()
-            store_res(a)
-            interleave("scalar", res_bf[a][0], res[a], 0)
-            interleave("scalar" if a < GROUPS - 1 else "vector", res_bf[a][1], res[a], 1)
+
+        def passes(a, first, last):
+            for h, j in order[first:last]:
+                fp4_passes(a, h, j)
+                fp8_pass(a, h, j)
+
+        banks_per_group = len(order)
+        adds(0, 0, 2)
+        quantize_w8(1)
+        passes(1, 0, 2)
+        for step in range(2, banks_per_group):
+            adds(0, step, step + 1)
+            passes(1, step, step + 1)
+        store_res(0)
+        interleave("scalar", res_bf[0][0], res[0], 0)
+        quantize_w8(2)
+        interleave("vector", res_bf[0][1], res[0], 1)
+        for step in range(banks_per_group):
+            adds(1, step, step + 1)
+            passes(2, step, step + 1)
+        store_res(1)
+        interleave("scalar", res_bf[1][0], res[1], 0)
+        quantize_res(0, 1)
+        quantize_res(0, 0)
+        store_codes(0)
+        store_first_scales()
+        adds(2, 0, banks_per_group)
+        store_res(2)
+        interleave("scalar", res_bf[2][0], res[2], 0)
+        interleave("vector", res_bf[1][1], res[1], 1)
+        quantize_res(1, 0)
+        interleave("vector", res_bf[2][1], res[2], 1)
         quantize_res(1, 1)
         store_codes(1)
         quantize_res(2, 1)

@@ -67,18 +67,18 @@ def tile_mix_atom_fm_pl_res_kernel(
             else:
                 nc.scalar.copy(out=out, in_=in_)
 
-        def interleave(engine, dst, src, h):
+        def interleave(engine, dst, src, h, c0=0, c1=N):
             copy_on(
                 engine,
-                dst[:].rearrange("p (c e i) -> p c i e", e=4, i=PACK),
-                src[:, :, h * N : (h + 1) * N].rearrange("p i (c e) -> p c i e", e=4),
+                dst[:, PACK * c0 : PACK * c1].rearrange("p (c e i) -> p c i e", e=4, i=PACK),
+                src[:, :, h * N + c0 : h * N + c1].rearrange("p i (c e) -> p c i e", e=4),
             )
 
-        def deal_w8(engine, a, j0=0, j1=PACK):
+        def deal_w8(engine, a):
             copy_on(
                 engine,
-                w8_bf[a][:].rearrange("p (j m i) -> p m j i", j=PACK, i=PACK)[:, :, j0:j1],
-                w8_raw[:, :, a * SPAN : (a + 1) * SPAN].rearrange("p i (m j) -> p m j i", j=PACK)[:, :, j0:j1],
+                w8_bf[a][:].rearrange("p (u v m i) -> p u m i v", u=2, v=2, i=PACK),
+                w8_raw[:, :, a * SPAN : (a + 1) * SPAN].rearrange("p i (m u v) -> p u m i v", u=2, v=2),
             )
 
         def deal_w4_words(a):
@@ -167,9 +167,9 @@ def tile_mix_atom_fm_pl_res_kernel(
         load_scales(nc.gpsimd, x4_s, x4_scales)
         nc.sync.dma_start(out=w4_w_raw[:].bitcast(I32), in_=w4_words.rearrange("g p b -> p g b").bitcast(I32))
         load_scales(nc.sync, w4_s_raw, w4_scales)
-        nc.sync.dma_start(out=x8_raw[:], in_=x8.rearrange("(p i) t -> p i t", i=PACK))
         nc.sync.dma_start(out=x4_w[:].bitcast(I32), in_=x4_words.rearrange("g p b -> p g b").bitcast(I32))
         nc.sync.dma_start(out=w8_raw[:], in_=w8.rearrange("(p i) n -> p i n", i=PACK))
+        nc.sync.dma_start(out=x8_raw[:], in_=x8.rearrange("(p i) t -> p i t", i=PACK))
         for j in range(0, PACK, 2):
             nc.sync.dma_start(out=res[0][:, j : j + 2, :], in_=rows_of(r, 0)[:, j : j + 2, :])
         for a in range(1, GROUPS):
@@ -180,32 +180,31 @@ def tile_mix_atom_fm_pl_res_kernel(
             deal_w4_scales(a)
         for h, j in order:
             fp4_passes(0, h, j)
+        deal_w8("vector", 0)
+        deal_w8("scalar", 2)
+        deal_w8("vector", 1)
+        quantize_w8(0)
+        quantize_w8(1)
         interleave("vector", x8_bf[0], x8_raw, 0)
-        interleave("scalar", x8_bf[1], x8_raw, 1)
+        interleave("scalar", x8_bf[1], x8_raw, 1, 0, N // 2)
+        interleave("vector", x8_bf[1], x8_raw, 1, N // 2, N)
         quantize_x8(0)
         quantize_x8(1)
-        deal_w8("vector", 0, 0, 3)
-        deal_w8("scalar", 0, 3, 4)
-        deal_w8("scalar", 1)
-        deal_w8("scalar", 2)
-        quantize_w8(0)
-        for h, j in order:
+        first_order = [(h, j) for pair in range(2) for h in range(HALVES) for j in (2 * pair, 2 * pair + 1)]
+        for h, j in first_order:
             fp8_pass(0, h, j)
 
         def adds(a, first, last):
-            for h, j in order[first:last]:
+            for h, j in first_order[first:last]:
                 add_residual(a, h, j)
 
         def passes(a, first, last):
-            for h, j in order[first:last]:
+            for h, j in first_order[first:last]:
                 fp4_passes(a, h, j)
                 fp8_pass(a, h, j)
 
         banks_per_group = len(order)
-        adds(0, 0, 2)
-        quantize_w8(1)
-        passes(1, 0, 2)
-        for step in range(2, banks_per_group):
+        for step in range(banks_per_group):
             adds(0, step, step + 1)
             passes(1, step, step + 1)
         store_res(0)

@@ -170,9 +170,7 @@ def tile_mix_atom_fm_pl_res_kernel(
         nc.sync.dma_start(out=x4_w[:].bitcast(I32), in_=x4_words.rearrange("g p b -> p g b").bitcast(I32))
         nc.sync.dma_start(out=w8_raw[:], in_=w8.rearrange("(p i) n -> p i n", i=PACK))
         nc.sync.dma_start(out=x8_raw[:], in_=x8.rearrange("(p i) t -> p i t", i=PACK))
-        for j in range(0, PACK, 2):
-            nc.sync.dma_start(out=res[0][:, j : j + 2, :], in_=rows_of(r, 0)[:, j : j + 2, :])
-        for a in range(1, GROUPS):
+        for a in range(GROUPS):
             nc.sync.dma_start(out=res[a][:], in_=rows_of(r, a))
 
         for a in range(GROUPS):
@@ -190,7 +188,8 @@ def tile_mix_atom_fm_pl_res_kernel(
         interleave("vector", x8_bf[1], x8_raw, 1, N // 2, N)
         quantize_x8(0)
         quantize_x8(1)
-        first_order = [(h, j) for pair in range(2) for h in range(HALVES) for j in (2 * pair, 2 * pair + 1)]
+        quantize_w8(2)
+        first_order = [(h, j) for h in range(HALVES) for j in range(PACK)]
         for h, j in first_order:
             fp8_pass(0, h, j)
 
@@ -209,21 +208,21 @@ def tile_mix_atom_fm_pl_res_kernel(
             passes(1, step, step + 1)
         store_res(0)
         interleave("scalar", res_bf[0][0], res[0], 0)
-        quantize_w8(2)
-        interleave("vector", res_bf[0][1], res[0], 1)
+        interleave("scalar", res_bf[0][1], res[0], 1, 0, N // 2)
+        interleave("vector", res_bf[0][1], res[0], 1, N // 2, N)
         for step in range(banks_per_group):
             adds(1, step, step + 1)
             passes(2, step, step + 1)
         store_res(1)
         interleave("scalar", res_bf[1][0], res[1], 0)
-        quantize_res(0, 1)
+        interleave("scalar", res_bf[1][1], res[1], 1)
         quantize_res(0, 0)
+        quantize_res(0, 1)
         store_codes(0)
         store_first_scales()
         adds(2, 0, banks_per_group)
         store_res(2)
         interleave("scalar", res_bf[2][0], res[2], 0)
-        interleave("vector", res_bf[1][1], res[1], 1)
         quantize_res(1, 0)
         interleave("vector", res_bf[2][1], res[2], 1)
         quantize_res(1, 1)

@@ -157,8 +157,8 @@ def tile_mix_atom_fm_pl_res_kernel(
                     in_=late_s[32 * q + 8 : 32 * q + 16, :].bitcast(I32),
                 )
 
-        def store_res(a):
-            nc.sync.dma_start(out=rows_of(out_0, a), in_=res[a][:])
+        def store_res(a, j0=0, j1=PACK):
+            nc.sync.dma_start(out=rows_of(out_0, a)[:, j0:j1, :], in_=res[a][:, j0:j1, :])
 
         order = [(h, j) for j in range(PACK) for h in range(HALVES)]
 
@@ -189,7 +189,7 @@ def tile_mix_atom_fm_pl_res_kernel(
         quantize_x8(0)
         quantize_x8(1)
         quantize_w8(2)
-        first_order = [(h, j) for h in range(HALVES) for j in range(PACK)]
+        first_order = [(h, j) for pair in range(2) for h in range(HALVES) for j in (2 * pair, 2 * pair + 1)]
         for h, j in first_order:
             fp8_pass(0, h, j)
 
@@ -206,7 +206,9 @@ def tile_mix_atom_fm_pl_res_kernel(
         for step in range(banks_per_group):
             adds(0, step, step + 1)
             passes(1, step, step + 1)
-        store_res(0)
+            if step == banks_per_group // 2 - 1:
+                store_res(0, 0, 2)
+        store_res(0, 2, 4)
         interleave("scalar", res_bf[0][0], res[0], 0)
         interleave("scalar", res_bf[0][1], res[0], 1, 0, N // 2)
         interleave("vector", res_bf[0][1], res[0], 1, N // 2, N)
@@ -220,8 +222,10 @@ def tile_mix_atom_fm_pl_res_kernel(
         quantize_res(0, 1)
         store_codes(0)
         store_first_scales()
-        adds(2, 0, banks_per_group)
-        store_res(2)
+        adds(2, 0, banks_per_group // 2)
+        store_res(2, 0, 2)
+        adds(2, banks_per_group // 2, banks_per_group)
+        store_res(2, 2, 4)
         interleave("scalar", res_bf[2][0], res[2], 0)
         quantize_res(1, 0)
         interleave("vector", res_bf[2][1], res[2], 1)

@@ -22,6 +22,7 @@ N = 512
 GROUPS = M // SPAN
 HALVES = T // N
 PASSES4 = K4 // SPAN
+ALIGN = 256
 
 
 def tile_mix_atom_fm_pl_res_kernel(
@@ -34,10 +35,10 @@ def tile_mix_atom_fm_pl_res_kernel(
         ctx.enter_context(tc.manual_schedule())
 
         def sb(name, shape, dtype):
-            return keep.tile(shape, dtype, name=name, align_bytes=64)
+            return keep.tile(shape, dtype, name=name, align_bytes=ALIGN)
 
-        x8_raw = sb("x8_raw", [P, PACK, T], F32)
-        w8_raw = sb("w8_raw", [P, PACK, M], F32)
+        x8_raw = sb("x8_raw", [P, PACK * T], F32)
+        w8_raw = sb("w8_raw", [P, PACK * M], F32)
         x4_w = sb("x4_w", [P, PASSES4, 2 * T], U8)
         x4_s = sb("x4_s", [P, PASSES4, T], U8)
         w4_w_raw = sb("w4_w_raw", [P, PASSES4, 2 * M], U8)
@@ -47,19 +48,19 @@ def tile_mix_atom_fm_pl_res_kernel(
         x8_bf = [sb(f"x8_bf{h}", [P, PACK * N], BF16) for h in range(HALVES)]
         x8_c = [sb(f"x8_c{h}", [P, N], U32) for h in range(HALVES)]
         x8_s = [sb(f"x8_s{h}", [P, N], U8) for h in range(HALVES)]
-        w8_bf = [sb(f"w8_bf{a}", [P, PACK * SPAN], BF16) for a in range(GROUPS)]
-        w8_c = [sb(f"w8_c{a}", [P, SPAN], U32) for a in range(GROUPS)]
-        w8_s = [sb(f"w8_s{a}", [P, SPAN], U8) for a in range(GROUPS)]
-        res = [sb(f"res{a}", [P, PACK, T], F32) for a in range(GROUPS)]
+        w8_bf = [[sb(f"w8_bf{a}_{u}", [P, 2 * SPAN], BF16) for u in range(2)] for a in range(GROUPS)]
+        w8_c = [[sb(f"w8_c{a}_{u}", [P, 2 * P], U32) for u in range(2)] for a in range(GROUPS)]
+        w8_s = [[sb(f"w8_s{a}_{u}", [P, 2 * P], U8) for u in range(2)] for a in range(GROUPS)]
+        res = [sb(f"res{a}", [P, PACK * T], F32) for a in range(GROUPS)]
         res_bf = [[sb(f"res_bf{a}_{h}", [P, PACK * N], BF16) for h in range(HALVES)] for a in range(GROUPS)]
         out_c = [sb(f"out_c{a}", [P, T], U32) for a in range(GROUPS)]
         first_s = sb("first_s", [P, T], U8)
-        late_s = sb("late_s", [P, T], U8)
-        out_s = [first_s, late_s, late_s]
+        late_s = sb("late_s", [P, GROUPS - 1, T], U8)
+        out_s = [first_s[4:P, :], late_s[8:P, 0, :], late_s[8:P, 1, :]]
         banks = {}
 
         def rows_of(dram, a):
-            return dram[a * SPAN : (a + 1) * SPAN, :].rearrange("(p j) t -> p j t", j=PACK)
+            return dram[a * SPAN : (a + 1) * SPAN, :].rearrange("(p j) t -> p (j t)", j=PACK)
 
         def copy_on(engine, out, in_):
             if engine == "vector":
@@ -68,17 +69,19 @@ def tile_mix_atom_fm_pl_res_kernel(
                 nc.scalar.copy(out=out, in_=in_)
 
         def interleave(engine, dst, src, h, c0=0, c1=N):
+            rows = src[:].rearrange("p (i t) -> p i t", i=PACK)
             copy_on(
                 engine,
                 dst[:, PACK * c0 : PACK * c1].rearrange("p (c e i) -> p c i e", e=4, i=PACK),
-                src[:, :, h * N + c0 : h * N + c1].rearrange("p i (c e) -> p c i e", e=4),
+                rows[:, :, h * N + c0 : h * N + c1].rearrange("p i (c e) -> p c i e", e=4),
             )
 
-        def deal_w8(engine, a):
+        def deal_w8(engine, a, u):
+            rows = w8_raw[:].rearrange("p (i n) -> p i n", i=PACK)
             copy_on(
                 engine,
-                w8_bf[a][:].rearrange("p (u v m i) -> p u m i v", u=2, v=2, i=PACK),
-                w8_raw[:, :, a * SPAN : (a + 1) * SPAN].rearrange("p i (m u v) -> p u m i v", u=2, v=2),
+                w8_bf[a][u][:].rearrange("p (v m i) -> p m i v", v=2, i=PACK),
+                rows[:, :, a * SPAN : (a + 1) * SPAN].rearrange("p i (m u v) -> p u m i v", u=2, v=2)[:, u],
             )
 
         def deal_w4_words(a):
@@ -96,15 +99,15 @@ def tile_mix_atom_fm_pl_res_kernel(
         def quantize(codes, scales, values):
             nc.vector.quantize_mx(out=codes.bitcast(FP8X4), scales=scales, in_=values)
 
-        def quantize_w8(a):
-            quantize(w8_c[a][:], w8_s[a][:], w8_bf[a][:])
+        def quantize_w8(a, u):
+            quantize(w8_c[a][u][:], w8_s[a][u][:], w8_bf[a][u][:])
 
         def quantize_x8(h):
             quantize(x8_c[h][:], x8_s[h][:], x8_bf[h][:])
 
         def quantize_res(a, h):
             cols = slice(h * N, (h + 1) * N)
-            quantize(out_c[a][:, cols], out_s[a][4 * (a + 1) : P, cols], res_bf[a][h][:])
+            quantize(out_c[a][:, cols], out_s[a][:, cols], res_bf[a][h][:])
 
         def fp4_passes(a, h, j):
             banks[a, h, j] = psum.tile([P, N], F32, name=f"bank{h}_{j}")
@@ -120,10 +123,11 @@ def tile_mix_atom_fm_pl_res_kernel(
                 )
 
         def fp8_pass(a, h, j):
+            u, v = divmod(j, 2)
             nc.tensor.matmul_mx(
                 out=banks[a, h, j][:],
-                lhsT=w8_c[a][:, j * P : (j + 1) * P].bitcast(FP8X4),
-                lhsT_scale=w8_s[a][:, j * P : (j + 1) * P],
+                lhsT=w8_c[a][u][:, v * P : (v + 1) * P].bitcast(FP8X4),
+                lhsT_scale=w8_s[a][u][:, v * P : (v + 1) * P],
                 rhs=x8_c[h][:].bitcast(FP8X4),
                 rhs_scale=x8_s[h][:],
                 start=False,
@@ -131,13 +135,12 @@ def tile_mix_atom_fm_pl_res_kernel(
             )
 
         def add_residual(a, h, j):
-            part = res[a][:, j, h * N : (h + 1) * N]
+            part = res[a][:, j * T + h * N : j * T + (h + 1) * N]
             nc.vector.tensor_tensor(out=part, in0=banks[a, h, j][:], in1=part, op=ADD)
 
-        def load_scales(queue, plane, dram):
+        def load_scale_rows(queue, plane, dram, s):
             by_row = dram.rearrange("g (q s) n -> s q g n", s=4)
-            for s in range(4):
-                queue.dma_start(out=plane[s:P:32].bitcast(I32), in_=by_row[s].bitcast(I32))
+            queue.dma_start(out=plane[s:P:32].bitcast(I32), in_=by_row[s].bitcast(I32))
 
         def store_codes(a):
             nc.sync.dma_start(
@@ -145,93 +148,89 @@ def tile_mix_atom_fm_pl_res_kernel(
                 in_=out_c[a][:].bitcast(I32),
             )
 
-        def store_first_scales():
+        def store_first_scales(queue):
             by_row = out_2[0].rearrange("(q s) n -> s q n", s=4)
             for s in range(4):
-                nc.gpsimd.dma_start(out=by_row[s].bitcast(I32), in_=first_s[4 + s : P : 32].bitcast(I32))
+                queue.dma_start(out=by_row[s].bitcast(I32), in_=first_s[4 + s : P : 32].bitcast(I32))
 
-        def store_late_scales():
-            for q in range(4):
-                nc.sync.dma_start(
-                    out=out_2[1:3, 4 * q : 4 * q + 4, :].bitcast(I32),
-                    in_=late_s[32 * q + 8 : 32 * q + 16, :].bitcast(I32),
-                )
+        def store_late_scales(queue):
+            by_row = out_2[1:GROUPS].rearrange("a (q s) n -> s q a n", s=4)
+            for s in range(4):
+                queue.dma_start(out=by_row[s].bitcast(I32), in_=late_s[8 + s : P : 32].bitcast(I32))
 
-        def store_res(a, j0=0, j1=PACK):
-            nc.sync.dma_start(out=rows_of(out_0, a)[:, j0:j1, :], in_=res[a][:, j0:j1, :])
-
-        order = [(h, j) for j in range(PACK) for h in range(HALVES)]
+        def store_res(a):
+            nc.sync.dma_start(out=rows_of(out_0, a), in_=res[a][:])
 
         nc.vector.memset(x4_s[:].rearrange("p g n -> p (g n)").bitcast(I32), 0)
         nc.vector.memset(w4_s_raw[:].rearrange("p g n -> p (g n)").bitcast(I32), 0)
-        load_scales(nc.gpsimd, x4_s, x4_scales)
         nc.sync.dma_start(out=w4_w_raw[:].bitcast(I32), in_=w4_words.rearrange("g p b -> p g b").bitcast(I32))
-        load_scales(nc.sync, w4_s_raw, w4_scales)
         nc.sync.dma_start(out=x4_w[:].bitcast(I32), in_=x4_words.rearrange("g p b -> p g b").bitcast(I32))
-        nc.sync.dma_start(out=w8_raw[:], in_=w8.rearrange("(p i) n -> p i n", i=PACK))
-        nc.sync.dma_start(out=x8_raw[:], in_=x8.rearrange("(p i) t -> p i t", i=PACK))
+        for s in range(4):
+            load_scale_rows(nc.sync, x4_s, x4_scales, s)
+        nc.sync.dma_start(out=x8_raw[:], in_=x8.rearrange("(p i) t -> p (i t)", i=PACK))
+        for s in range(4):
+            load_scale_rows(nc.sync, w4_s_raw, w4_scales, s)
+        nc.sync.dma_start(out=w8_raw[:], in_=w8.rearrange("(p i) n -> p (i n)", i=PACK))
         for a in range(GROUPS):
             nc.sync.dma_start(out=res[a][:], in_=rows_of(r, a))
 
         for a in range(GROUPS):
             deal_w4_words(a)
-            deal_w4_scales(a)
+        interleave("scalar", x8_bf[1], x8_raw, 1)
+        interleave("vector", x8_bf[0], x8_raw, 0)
+        deal_w4_scales(0)
+        order = [(h, j) for j in range(PACK) for h in range(HALVES)]
         for h, j in order:
             fp4_passes(0, h, j)
-        deal_w8("vector", 0)
-        deal_w8("scalar", 2)
-        deal_w8("vector", 1)
-        quantize_w8(0)
-        quantize_w8(1)
-        interleave("vector", x8_bf[0], x8_raw, 0)
-        interleave("scalar", x8_bf[1], x8_raw, 1, 0, N // 2)
-        interleave("vector", x8_bf[1], x8_raw, 1, N // 2, N)
         quantize_x8(0)
+        for a in range(1, GROUPS):
+            deal_w4_scales(a)
         quantize_x8(1)
-        quantize_w8(2)
-        first_order = [(h, j) for pair in range(2) for h in range(HALVES) for j in (2 * pair, 2 * pair + 1)]
-        for h, j in first_order:
+
+        deal_w8("vector", 0, 0)
+        deal_w8("scalar", 0, 1)
+        quantize_w8(0, 0)
+        deal_w8("vector", 1, 0)
+        quantize_w8(0, 1)
+        for h, j in order:
             fp8_pass(0, h, j)
+        deal_w8("vector", 1, 1)
+        deal_w8("scalar", 2, 0)
+        deal_w8("scalar", 2, 1)
+        quantize_w8(1, 0)
+        quantize_w8(1, 1)
 
-        def adds(a, first, last):
-            for h, j in first_order[first:last]:
+        def adds_and_next_passes(a, steps):
+            for h, j in steps:
                 add_residual(a, h, j)
+                if a + 1 < GROUPS:
+                    fp4_passes(a + 1, h, j)
+                    fp8_pass(a + 1, h, j)
 
-        def passes(a, first, last):
-            for h, j in first_order[first:last]:
-                fp4_passes(a, h, j)
-                fp8_pass(a, h, j)
+        def adds_with_interleave(a):
+            adds_and_next_passes(a, order[:-1])
+            interleave("scalar", res_bf[a][0], res[a], 0)
+            adds_and_next_passes(a, order[-1:])
 
-        banks_per_group = len(order)
-        for step in range(banks_per_group):
-            adds(0, step, step + 1)
-            passes(1, step, step + 1)
-            if step == banks_per_group // 2 - 1:
-                store_res(0, 0, 2)
-        store_res(0, 2, 4)
-        interleave("scalar", res_bf[0][0], res[0], 0)
-        interleave("scalar", res_bf[0][1], res[0], 1, 0, N // 2)
-        interleave("vector", res_bf[0][1], res[0], 1, N // 2, N)
-        for step in range(banks_per_group):
-            adds(1, step, step + 1)
-            passes(2, step, step + 1)
-        store_res(1)
-        interleave("scalar", res_bf[1][0], res[1], 0)
+        adds_with_interleave(0)
+        interleave("scalar", res_bf[0][1], res[0], 1)
+        store_res(0)
+        quantize_w8(2, 0)
+        quantize_w8(2, 1)
+        adds_with_interleave(1)
         interleave("scalar", res_bf[1][1], res[1], 1)
+        store_res(1)
         quantize_res(0, 0)
         quantize_res(0, 1)
         store_codes(0)
-        store_first_scales()
-        adds(2, 0, banks_per_group // 2)
-        store_res(2, 0, 2)
-        adds(2, banks_per_group // 2, banks_per_group)
-        store_res(2, 2, 4)
-        interleave("scalar", res_bf[2][0], res[2], 0)
+        store_first_scales(nc.sync)
+        adds_with_interleave(2)
+        store_res(2)
         quantize_res(1, 0)
         interleave("vector", res_bf[2][1], res[2], 1)
         quantize_res(1, 1)
         store_codes(1)
         quantize_res(2, 1)
         quantize_res(2, 0)
-        store_late_scales()
+        store_late_scales(nc.sync)
         store_codes(2)

@@ -43,6 +43,7 @@ def tile_mix_atom_fm_pl_res_kernel(
         x4_s = sb("x4_s", [P, PASSES4, T], U8)
         w4_w_raw = sb("w4_w_raw", [P, PASSES4, 2 * M], U8)
         w4_s_raw = sb("w4_s_raw", [P, PASSES4, M], U8)
+        x4_s_in = sb("x4_s_in", [P, PASSES4, T], U8)
         w4_w = [sb(f"w4_w{a}", [P, PASSES4, PACK, 2 * P], U8) for a in range(GROUPS)]
         w4_s = [sb(f"w4_s{a}", [P, PASSES4, PACK, P], U8) for a in range(GROUPS)]
         x8_bf = [sb(f"x8_bf{h}", [P, PACK * N], BF16) for h in range(HALVES)]
@@ -142,6 +143,12 @@ def tile_mix_atom_fm_pl_res_kernel(
             by_row = dram.rearrange("g (q s) n -> s q g n", s=4)
             queue.dma_start(out=plane[s:P:32].bitcast(I32), in_=by_row[s].bitcast(I32))
 
+        def place_scale_rows(plane, landed):
+            words = plane[:].rearrange("p g n -> p (g n)").bitcast(I32)
+            for q in range(4):
+                live = slice(32 * q, 32 * q + 4)
+                nc.vector.tensor_copy(out=words[live], in_=landed[:].rearrange("p g n -> p (g n)").bitcast(I32)[live])
+
         def store_codes(a):
             nc.sync.dma_start(
                 out=out_1[a].rearrange("p t b -> p (t b)").bitcast(I32),
@@ -161,31 +168,32 @@ def tile_mix_atom_fm_pl_res_kernel(
         def store_res(a):
             nc.sync.dma_start(out=rows_of(out_0, a), in_=res[a][:])
 
-        nc.vector.memset(x4_s[:].rearrange("p g n -> p (g n)").bitcast(I32), 0)
         nc.vector.memset(w4_s_raw[:].rearrange("p g n -> p (g n)").bitcast(I32), 0)
+        nc.vector.memset(x4_s[:].rearrange("p g n -> p (g n)").bitcast(I32), 0)
+        for s in range(4):
+            load_scale_rows(nc.scalar, x4_s_in, x4_scales, s)
         nc.sync.dma_start(out=w4_w_raw[:].bitcast(I32), in_=w4_words.rearrange("g p b -> p g b").bitcast(I32))
         nc.sync.dma_start(out=x4_w[:].bitcast(I32), in_=x4_words.rearrange("g p b -> p g b").bitcast(I32))
-        for s in range(4):
-            load_scale_rows(nc.sync, x4_s, x4_scales, s)
         nc.sync.dma_start(out=x8_raw[:], in_=x8.rearrange("(p i) t -> p (i t)", i=PACK))
         for s in range(4):
-            load_scale_rows(nc.sync, w4_s_raw, w4_scales, s)
+            load_scale_rows(nc.scalar, w4_s_raw, w4_scales, s)
         nc.sync.dma_start(out=w8_raw[:], in_=w8.rearrange("(p i) n -> p (i n)", i=PACK))
         for a in range(GROUPS):
             nc.sync.dma_start(out=res[a][:], in_=rows_of(r, a))
 
         for a in range(GROUPS):
             deal_w4_words(a)
+        place_scale_rows(x4_s, x4_s_in)
         interleave("scalar", x8_bf[1], x8_raw, 1)
         interleave("vector", x8_bf[0], x8_raw, 0)
+        quantize_x8(0)
+        quantize_x8(1)
         deal_w4_scales(0)
         order = [(h, j) for j in range(PACK) for h in range(HALVES)]
         for h, j in order:
             fp4_passes(0, h, j)
-        quantize_x8(0)
         for a in range(1, GROUPS):
             deal_w4_scales(a)
-        quantize_x8(1)
 
         deal_w8("vector", 0, 0)
         deal_w8("scalar", 0, 1)

@@ -55,9 +55,8 @@ def tile_mix_atom_fm_pl_res_kernel(
         res = [sb(f"res{a}", [P, PACK * T], F32) for a in range(GROUPS)]
         res_bf = [[sb(f"res_bf{a}_{h}", [P, PACK * N], BF16) for h in range(HALVES)] for a in range(GROUPS)]
         out_c = [sb(f"out_c{a}", [P, T], U32) for a in range(GROUPS)]
-        first_s = sb("first_s", [P, T], U8)
-        late_s = sb("late_s", [P, GROUPS - 1, T], U8)
-        out_s = [first_s[4:P, :], late_s[8:P, 0, :], late_s[8:P, 1, :]]
+        planes = sb("planes", [P, T], U8)
+        out_s = [planes[4 * a : P, :] for a in range(GROUPS)]
         banks = {}
 
         def rows_of(dram, a):
@@ -155,15 +154,12 @@ def tile_mix_atom_fm_pl_res_kernel(
                 in_=out_c[a][:].bitcast(I32),
             )
 
-        def store_first_scales(queue):
-            by_row = out_2[0].rearrange("(q s) n -> s q n", s=4)
-            for s in range(4):
-                queue.dma_start(out=by_row[s].bitcast(I32), in_=first_s[4 + s : P : 32].bitcast(I32))
-
-        def store_late_scales(queue):
-            by_row = out_2[1:GROUPS].rearrange("a (q s) n -> s q a n", s=4)
-            for s in range(4):
-                queue.dma_start(out=by_row[s].bitcast(I32), in_=late_s[8 + s : P : 32].bitcast(I32))
+        def store_scales():
+            for q in range(4):
+                nc.sync.dma_start(
+                    out=out_2[:, 4 * q : 4 * q + 4, :].bitcast(I32),
+                    in_=planes[32 * q : 32 * q + 4 * GROUPS, :].bitcast(I32),
+                )
 
         def store_res(a):
             nc.sync.dma_start(out=rows_of(out_0, a), in_=res[a][:])
@@ -231,7 +227,6 @@ def tile_mix_atom_fm_pl_res_kernel(
         quantize_res(0, 0)
         quantize_res(0, 1)
         store_codes(0)
-        store_first_scales(nc.sync)
         adds_with_interleave(2)
         store_res(2)
         quantize_res(1, 0)
@@ -240,5 +235,5 @@ def tile_mix_atom_fm_pl_res_kernel(
         store_codes(1)
         quantize_res(2, 1)
         quantize_res(2, 0)
-        store_late_scales(nc.sync)
         store_codes(2)
+        store_scales()

@@ -156,7 +156,8 @@ def tile_mix_atom_fm_pl_res_kernel(
 
         def store_scales():
             for q in range(4):
-                nc.sync.dma_start(
+                queue = nc.sync if q < 2 else nc.scalar
+                queue.dma_start(
                     out=out_2[:, 4 * q : 4 * q + 4, :].bitcast(I32),
                     in_=planes[32 * q : 32 * q + 4 * GROUPS, :].bitcast(I32),
                 )

@@ -110,7 +110,6 @@ def tile_mix_atom_fm_pl_res_kernel(
             quantize(out_c[a][:, cols], out_s[a][:, cols], res_bf[a][h][:])
 
         def fp4_passes(a, h, j):
-            banks[a, h, j] = psum.tile([P, N], F32, name=f"bank{h}_{j}")
             for g in range(PASSES4):
                 nc.tensor.matmul_mx(
                     out=banks[a, h, j][:],
@@ -118,20 +117,21 @@ def tile_mix_atom_fm_pl_res_kernel(
                     lhsT_scale=w4_s[a][:, g, j, :],
                     rhs=x4_w[:, g, 2 * N * h : 2 * N * (h + 1)].bitcast(FP4X4),
                     rhs_scale=x4_s[:, g, N * h : N * (h + 1)],
-                    start=(g == 0),
-                    stop=False,
+                    start=False,
+                    stop=(g == PASSES4 - 1),
                 )
 
         def fp8_pass(a, h, j):
             u, v = divmod(j, 2)
+            banks[a, h, j] = psum.tile([P, N], F32, name=f"bank{h}_{j}")
             nc.tensor.matmul_mx(
                 out=banks[a, h, j][:],
                 lhsT=w8_c[a][u][:, v * P : (v + 1) * P].bitcast(FP8X4),
                 lhsT_scale=w8_s[a][u][:, v * P : (v + 1) * P],
                 rhs=x8_c[h][:].bitcast(FP8X4),
                 rhs_scale=x8_s[h][:],
-                start=False,
-                stop=True,
+                start=True,
+                stop=False,
             )
 
         def add_residual(a, h, j):
@@ -169,48 +169,49 @@ def tile_mix_atom_fm_pl_res_kernel(
         nc.vector.memset(x4_s[:].rearrange("p g n -> p (g n)").bitcast(I32), 0)
         for s in range(4):
             load_scale_rows(nc.scalar, x4_s_in, x4_scales, s)
+        nc.sync.dma_start(out=x8_raw[:], in_=x8.rearrange("(p i) t -> p (i t)", i=PACK))
+        nc.sync.dma_start(out=w8_raw[:], in_=w8.rearrange("(p i) n -> p (i n)", i=PACK))
         nc.sync.dma_start(out=w4_w_raw[:].bitcast(I32), in_=w4_words.rearrange("g p b -> p g b").bitcast(I32))
         nc.sync.dma_start(out=x4_w[:].bitcast(I32), in_=x4_words.rearrange("g p b -> p g b").bitcast(I32))
-        nc.sync.dma_start(out=x8_raw[:], in_=x8.rearrange("(p i) t -> p (i t)", i=PACK))
-        for s in range(4):
-            load_scale_rows(nc.scalar, w4_s_raw, w4_scales, s)
-        nc.sync.dma_start(out=w8_raw[:], in_=w8.rearrange("(p i) n -> p (i n)", i=PACK))
         for a in range(GROUPS):
             nc.sync.dma_start(out=res[a][:], in_=rows_of(r, a))
 
-        for a in range(GROUPS):
-            deal_w4_words(a)
-        place_scale_rows(x4_s, x4_s_in)
         interleave("scalar", x8_bf[1], x8_raw, 1)
+        for s in range(4):
+            load_scale_rows(nc.scalar, w4_s_raw, w4_scales, s)
         interleave("vector", x8_bf[0], x8_raw, 0)
         quantize_x8(0)
         quantize_x8(1)
-        deal_w4_scales(0)
-        order = [(h, j) for j in range(PACK) for h in range(HALVES)]
-        for h, j in order:
-            fp4_passes(0, h, j)
-        for a in range(1, GROUPS):
-            deal_w4_scales(a)
 
+        order = [(h, j) for j in range(PACK) for h in range(HALVES)]
         deal_w8("vector", 0, 0)
         deal_w8("scalar", 0, 1)
         quantize_w8(0, 0)
-        deal_w8("vector", 1, 0)
+        deal_w4_words(0)
         quantize_w8(0, 1)
         for h, j in order:
             fp8_pass(0, h, j)
-        deal_w8("vector", 1, 1)
+        place_scale_rows(x4_s, x4_s_in)
+        deal_w4_scales(0)
+        for h, j in order:
+            fp4_passes(0, h, j)
+        deal_w8("vector", 1, 0)
+        deal_w8("scalar", 1, 1)
         deal_w8("scalar", 2, 0)
         deal_w8("scalar", 2, 1)
-        quantize_w8(1, 0)
-        quantize_w8(1, 1)
+        for a in range(1, GROUPS):
+            deal_w4_words(a)
+            deal_w4_scales(a)
+        for a in range(1, GROUPS):
+            quantize_w8(a, 0)
+            quantize_w8(a, 1)
 
         def adds_and_next_passes(a, steps):
             for h, j in steps:
                 add_residual(a, h, j)
                 if a + 1 < GROUPS:
-                    fp4_passes(a + 1, h, j)
                     fp8_pass(a + 1, h, j)
+                    fp4_passes(a + 1, h, j)
 
         def adds_with_interleave(a):
             adds_and_next_passes(a, order[:-1])
@@ -220,8 +221,6 @@ def tile_mix_atom_fm_pl_res_kernel(
         adds_with_interleave(0)
         interleave("scalar", res_bf[0][1], res[0], 1)
         store_res(0)
-        quantize_w8(2, 0)
-        quantize_w8(2, 1)
         adds_with_interleave(1)
         interleave("scalar", res_bf[1][1], res[1], 1)
         store_res(1)

@@ -171,14 +171,14 @@ def tile_mix_atom_fm_pl_res_kernel(
             load_scale_rows(nc.scalar, x4_s_in, x4_scales, s)
         nc.sync.dma_start(out=x8_raw[:], in_=x8.rearrange("(p i) t -> p (i t)", i=PACK))
         nc.sync.dma_start(out=w8_raw[:], in_=w8.rearrange("(p i) n -> p (i n)", i=PACK))
+        for s in range(4):
+            load_scale_rows(nc.scalar if s < 2 else nc.sync, w4_s_raw, w4_scales, s)
         nc.sync.dma_start(out=w4_w_raw[:].bitcast(I32), in_=w4_words.rearrange("g p b -> p g b").bitcast(I32))
         nc.sync.dma_start(out=x4_w[:].bitcast(I32), in_=x4_words.rearrange("g p b -> p g b").bitcast(I32))
         for a in range(GROUPS):
             nc.sync.dma_start(out=res[a][:], in_=rows_of(r, a))
 
         interleave("scalar", x8_bf[1], x8_raw, 1)
-        for s in range(4):
-            load_scale_rows(nc.scalar, w4_s_raw, w4_scales, s)
         interleave("vector", x8_bf[0], x8_raw, 0)
         quantize_x8(0)
         quantize_x8(1)

@@ -43,7 +43,6 @@ def tile_mix_atom_fm_pl_res_kernel(
         x4_s = sb("x4_s", [P, PASSES4, T], U8)
         w4_w_raw = sb("w4_w_raw", [P, PASSES4, 2 * M], U8)
         w4_s_raw = sb("w4_s_raw", [P, PASSES4, M], U8)
-        x4_s_in = sb("x4_s_in", [P, PASSES4, T], U8)
         w4_w = [sb(f"w4_w{a}", [P, PASSES4, PACK, 2 * P], U8) for a in range(GROUPS)]
         w4_s = [sb(f"w4_s{a}", [P, PASSES4, PACK, P], U8) for a in range(GROUPS)]
         x8_bf = [sb(f"x8_bf{h}", [P, PACK * N], BF16) for h in range(HALVES)]
@@ -142,12 +141,6 @@ def tile_mix_atom_fm_pl_res_kernel(
             by_row = dram.rearrange("g (q s) n -> s q g n", s=4)
             queue.dma_start(out=plane[s:P:32].bitcast(I32), in_=by_row[s].bitcast(I32))
 
-        def place_scale_rows(plane, landed):
-            words = plane[:].rearrange("p g n -> p (g n)").bitcast(I32)
-            for q in range(4):
-                live = slice(32 * q, 32 * q + 4)
-                nc.vector.tensor_copy(out=words[live], in_=landed[:].rearrange("p g n -> p (g n)").bitcast(I32)[live])
-
         def store_codes(a):
             nc.sync.dma_start(
                 out=out_1[a].rearrange("p t b -> p (t b)").bitcast(I32),
@@ -165,14 +158,16 @@ def tile_mix_atom_fm_pl_res_kernel(
         def store_res(a):
             nc.sync.dma_start(out=rows_of(out_0, a), in_=res[a][:])
 
-        nc.vector.memset(w4_s_raw[:].rearrange("p g n -> p (g n)").bitcast(I32), 0)
         nc.vector.memset(x4_s[:].rearrange("p g n -> p (g n)").bitcast(I32), 0)
-        for s in range(4):
-            load_scale_rows(nc.scalar, x4_s_in, x4_scales, s)
+        nc.vector.memset(w4_s_raw[:].rearrange("p g n -> p (g n)").bitcast(I32), 0)
         nc.sync.dma_start(out=x8_raw[:], in_=x8.rearrange("(p i) t -> p (i t)", i=PACK))
-        nc.sync.dma_start(out=w8_raw[:], in_=w8.rearrange("(p i) n -> p (i n)", i=PACK))
         for s in range(4):
-            load_scale_rows(nc.scalar if s < 2 else nc.sync, w4_s_raw, w4_scales, s)
+            load_scale_rows(nc.sync, x4_s, x4_scales, s)
+        for s in range(2):
+            load_scale_rows(nc.sync, w4_s_raw, w4_scales, s)
+        nc.sync.dma_start(out=w8_raw[:], in_=w8.rearrange("(p i) n -> p (i n)", i=PACK))
+        for s in range(2, 4):
+            load_scale_rows(nc.sync, w4_s_raw, w4_scales, s)
         nc.sync.dma_start(out=w4_w_raw[:].bitcast(I32), in_=w4_words.rearrange("g p b -> p g b").bitcast(I32))
         nc.sync.dma_start(out=x4_w[:].bitcast(I32), in_=x4_words.rearrange("g p b -> p g b").bitcast(I32))
         for a in range(GROUPS):
@@ -191,7 +186,6 @@ def tile_mix_atom_fm_pl_res_kernel(
         quantize_w8(0, 1)
         for h, j in order:
             fp8_pass(0, h, j)
-        place_scale_rows(x4_s, x4_s_in)
         deal_w4_scales(0)
         for h, j in order:
             fp4_passes(0, h, j)

@@ -158,18 +158,23 @@ def tile_mix_atom_fm_pl_res_kernel(
         def store_res(a):
             nc.sync.dma_start(out=rows_of(out_0, a), in_=res[a][:])
 
-        nc.vector.memset(x4_s[:].rearrange("p g n -> p (g n)").bitcast(I32), 0)
         nc.vector.memset(w4_s_raw[:].rearrange("p g n -> p (g n)").bitcast(I32), 0)
+        nc.vector.memset(x4_s[:].rearrange("p g n -> p (g n)").bitcast(I32), 0)
+        def load_words(tile, dram, g):
+            nc.sync.dma_start(out=tile[:, g, :].bitcast(I32), in_=dram[g].bitcast(I32))
+
         nc.sync.dma_start(out=x8_raw[:], in_=x8.rearrange("(p i) t -> p (i t)", i=PACK))
-        for s in range(4):
-            load_scale_rows(nc.sync, x4_s, x4_scales, s)
-        for s in range(2):
-            load_scale_rows(nc.sync, w4_s_raw, w4_scales, s)
+        load_scale_rows(nc.sync, w4_s_raw, w4_scales, 0)
+        load_scale_rows(nc.sync, w4_s_raw, w4_scales, 1)
         nc.sync.dma_start(out=w8_raw[:], in_=w8.rearrange("(p i) n -> p (i n)", i=PACK))
-        for s in range(2, 4):
-            load_scale_rows(nc.sync, w4_s_raw, w4_scales, s)
-        nc.sync.dma_start(out=w4_w_raw[:].bitcast(I32), in_=w4_words.rearrange("g p b -> p g b").bitcast(I32))
-        nc.sync.dma_start(out=x4_w[:].bitcast(I32), in_=x4_words.rearrange("g p b -> p g b").bitcast(I32))
+        for g in range(PASSES4):
+            load_scale_rows(nc.sync, w4_s_raw, w4_scales, 2 + g)
+            load_words(w4_w_raw, w4_words, g)
+        for g in range(PASSES4):
+            load_scale_rows(nc.sync, x4_s, x4_scales, g)
+            load_words(x4_w, x4_words, g)
+        load_scale_rows(nc.sync, x4_s, x4_scales, 2)
+        load_scale_rows(nc.sync, x4_s, x4_scales, 3)
         for a in range(GROUPS):
             nc.sync.dma_start(out=res[a][:], in_=rows_of(r, a))
 

@@ -160,21 +160,18 @@ def tile_mix_atom_fm_pl_res_kernel(
 
         nc.vector.memset(w4_s_raw[:].rearrange("p g n -> p (g n)").bitcast(I32), 0)
         nc.vector.memset(x4_s[:].rearrange("p g n -> p (g n)").bitcast(I32), 0)
-        def load_words(tile, dram, g):
-            nc.sync.dma_start(out=tile[:, g, :].bitcast(I32), in_=dram[g].bitcast(I32))
+        def two_scale_loads(plane, dram, first):
+            load_scale_rows(nc.sync, plane, dram, first)
+            load_scale_rows(nc.sync, plane, dram, first + 1)
 
         nc.sync.dma_start(out=x8_raw[:], in_=x8.rearrange("(p i) t -> p (i t)", i=PACK))
-        load_scale_rows(nc.sync, w4_s_raw, w4_scales, 0)
-        load_scale_rows(nc.sync, w4_s_raw, w4_scales, 1)
+        two_scale_loads(w4_s_raw, w4_scales, 0)
         nc.sync.dma_start(out=w8_raw[:], in_=w8.rearrange("(p i) n -> p (i n)", i=PACK))
-        for g in range(PASSES4):
-            load_scale_rows(nc.sync, w4_s_raw, w4_scales, 2 + g)
-            load_words(w4_w_raw, w4_words, g)
-        for g in range(PASSES4):
-            load_scale_rows(nc.sync, x4_s, x4_scales, g)
-            load_words(x4_w, x4_words, g)
-        load_scale_rows(nc.sync, x4_s, x4_scales, 2)
-        load_scale_rows(nc.sync, x4_s, x4_scales, 3)
+        two_scale_loads(w4_s_raw, w4_scales, 2)
+        nc.sync.dma_start(out=w4_w_raw[:].bitcast(I32), in_=w4_words.rearrange("g p b -> p g b").bitcast(I32))
+        two_scale_loads(x4_s, x4_scales, 0)
+        nc.sync.dma_start(out=x4_w[:].bitcast(I32), in_=x4_words.rearrange("g p b -> p g b").bitcast(I32))
+        two_scale_loads(x4_s, x4_scales, 2)
         for a in range(GROUPS):
             nc.sync.dma_start(out=res[a][:], in_=rows_of(r, a))
 

@@ -217,18 +217,25 @@ def tile_mix_atom_fm_pl_res_kernel(
         adds_with_interleave(0)
         interleave("scalar", res_bf[0][1], res[0], 1)
         store_res(0)
-        adds_with_interleave(1)
+        adds_and_next_passes(1, order[:5])
+        quantize_res(0, 0)
+        adds_and_next_passes(1, order[5:7])
+        interleave("scalar", res_bf[1][0], res[1], 0)
+        adds_and_next_passes(1, order[7:])
         interleave("scalar", res_bf[1][1], res[1], 1)
         store_res(1)
-        quantize_res(0, 0)
         quantize_res(0, 1)
         store_codes(0)
-        adds_with_interleave(2)
-        store_res(2)
+        adds_and_next_passes(2, order[:4])
         quantize_res(1, 0)
-        interleave("vector", res_bf[2][1], res[2], 1)
+        adds_and_next_passes(2, order[4:6])
         quantize_res(1, 1)
         store_codes(1)
+        adds_and_next_passes(2, order[6:7])
+        interleave("scalar", res_bf[2][0], res[2], 0)
+        adds_and_next_passes(2, order[7:])
+        store_res(2)
+        interleave("vector", res_bf[2][1], res[2], 1)
         quantize_res(2, 1)
         quantize_res(2, 0)
         store_codes(2)

@@ -19,10 +19,12 @@ P = 128
 PACK = 4
 SPAN = P * PACK
 N = 512
+QUAD = 32
 GROUPS = M // SPAN
 HALVES = T // N
 PASSES4 = K4 // SPAN
 ALIGN = 256
+QUANTISE_AFTER = (4, 7)
 
 
 def tile_mix_atom_fm_pl_res_kernel(
@@ -40,7 +42,7 @@ def tile_mix_atom_fm_pl_res_kernel(
         x8_raw = sb("x8_raw", [P, PACK * T], F32)
         w8_raw = sb("w8_raw", [P, PACK * M], F32)
         x4_w = sb("x4_w", [P, PASSES4, 2 * T], U8)
-        x4_s = sb("x4_s", [P, PASSES4, T], U8)
+        x4_s = sb("x4_s", [P, PASSES4 * 2 * T], U8)
         w4_w_raw = sb("w4_w_raw", [P, PASSES4, 2 * M], U8)
         w4_s_raw = sb("w4_s_raw", [P, PASSES4, M], U8)
         w4_w = [sb(f"w4_w{a}", [P, PASSES4, PACK, 2 * P], U8) for a in range(GROUPS)]
@@ -55,7 +57,7 @@ def tile_mix_atom_fm_pl_res_kernel(
         res_bf = [[sb(f"res_bf{a}_{h}", [P, PACK * N], BF16) for h in range(HALVES)] for a in range(GROUPS)]
         out_c = [sb(f"out_c{a}", [P, T], U32) for a in range(GROUPS)]
         planes = sb("planes", [P, T], U8)
-        out_s = [planes[4 * a : P, :] for a in range(GROUPS)]
+        out_s = [planes[PACK * (a + 1) : P, :] for a in range(GROUPS)]
         banks = {}
 
         def rows_of(dram, a):
@@ -67,12 +69,12 @@ def tile_mix_atom_fm_pl_res_kernel(
             else:
                 nc.scalar.copy(out=out, in_=in_)
 
-        def interleave(engine, dst, src, h, c0=0, c1=N):
+        def interleave(engine, dst, src, h):
             rows = src[:].rearrange("p (i t) -> p i t", i=PACK)
             copy_on(
                 engine,
-                dst[:, PACK * c0 : PACK * c1].rearrange("p (c e i) -> p c i e", e=4, i=PACK),
-                rows[:, :, h * N + c0 : h * N + c1].rearrange("p i (c e) -> p c i e", e=4),
+                dst[:].rearrange("p (c e i) -> p c i e", e=4, i=PACK),
+                rows[:, :, h * N : (h + 1) * N].rearrange("p i (c e) -> p c i e", e=4),
             )
 
         def deal_w8(engine, a, u):
@@ -101,24 +103,9 @@ def tile_mix_atom_fm_pl_res_kernel(
         def quantize_w8(a, u):
             quantize(w8_c[a][u][:], w8_s[a][u][:], w8_bf[a][u][:])
 
-        def quantize_x8(h):
-            quantize(x8_c[h][:], x8_s[h][:], x8_bf[h][:])
-
         def quantize_res(a, h):
             cols = slice(h * N, (h + 1) * N)
             quantize(out_c[a][:, cols], out_s[a][:, cols], res_bf[a][h][:])
-
-        def fp4_passes(a, h, j):
-            for g in range(PASSES4):
-                nc.tensor.matmul_mx(
-                    out=banks[a, h, j][:],
-                    lhsT=w4_w[a][:, g, j, :].bitcast(FP4X4),
-                    lhsT_scale=w4_s[a][:, g, j, :],
-                    rhs=x4_w[:, g, 2 * N * h : 2 * N * (h + 1)].bitcast(FP4X4),
-                    rhs_scale=x4_s[:, g, N * h : N * (h + 1)],
-                    start=False,
-                    stop=(g == PASSES4 - 1),
-                )
 
         def fp8_pass(a, h, j):
             u, v = divmod(j, 2)
@@ -133,13 +120,40 @@ def tile_mix_atom_fm_pl_res_kernel(
                 stop=False,
             )
 
+        def fp4_passes(a, h, j):
+            for g in range(PASSES4):
+                first = (2 * g + 1) * T + N * h
+                nc.tensor.matmul_mx(
+                    out=banks[a, h, j][:],
+                    lhsT=w4_w[a][:, g, j, :].bitcast(FP4X4),
+                    lhsT_scale=w4_s[a][:, g, j, :],
+                    rhs=x4_w[:, g, 2 * N * h : 2 * N * (h + 1)].bitcast(FP4X4),
+                    rhs_scale=x4_s[:, first : first + N],
+                    start=False,
+                    stop=(g == PASSES4 - 1),
+                )
+
         def add_residual(a, h, j):
             part = res[a][:, j * T + h * N : j * T + (h + 1) * N]
             nc.vector.tensor_tensor(out=part, in0=banks[a, h, j][:], in1=part, op=ADD)
 
-        def load_scale_rows(queue, plane, dram, s):
-            by_row = dram.rearrange("g (q s) n -> s q g n", s=4)
-            queue.dma_start(out=plane[s:P:32].bitcast(I32), in_=by_row[s].bitcast(I32))
+        def load_w4_scale_rows(s):
+            by_row = w4_scales.rearrange("g (q s) n -> s q g n", s=4)
+            nc.sync.dma_start(out=w4_s_raw[s:P:QUAD].bitcast(I32), in_=by_row[s].bitcast(I32))
+
+        def load_x4_scale_rows(odd):
+            by_parity = x4_scales.rearrange("g (u o s) n -> o s (g u) n", o=2, s=4)
+            first = (2 + odd) * QUAD
+            nc.sync.dma_start(
+                out=x4_s[first : first + 4, :].rearrange("s (c n) -> s c n", n=T).bitcast(I32),
+                in_=by_parity[odd].bitcast(I32),
+            )
+
+        def spread_x4_scale_rows(g):
+            nc.vector.tensor_copy(
+                out=x4_s[0 : P // 2, (2 * g + 1) * T : (2 * g + 2) * T].bitcast(I32),
+                in_=x4_s[P // 2 : P, 2 * g * T : (2 * g + 1) * T].bitcast(I32),
+            )
 
         def store_codes(a):
             nc.sync.dma_start(
@@ -152,42 +166,42 @@ def tile_mix_atom_fm_pl_res_kernel(
                 queue = nc.sync if q < 2 else nc.scalar
                 queue.dma_start(
                     out=out_2[:, 4 * q : 4 * q + 4, :].bitcast(I32),
-                    in_=planes[32 * q : 32 * q + 4 * GROUPS, :].bitcast(I32),
+                    in_=planes[QUAD * q + PACK : QUAD * q + PACK * (GROUPS + 1), :].bitcast(I32),
                 )
 
         def store_res(a):
             nc.sync.dma_start(out=rows_of(out_0, a), in_=res[a][:])
 
+        nc.vector.memset(x4_s[:].bitcast(I32), 0)
         nc.vector.memset(w4_s_raw[:].rearrange("p g n -> p (g n)").bitcast(I32), 0)
-        nc.vector.memset(x4_s[:].rearrange("p g n -> p (g n)").bitcast(I32), 0)
-        def two_scale_loads(plane, dram, first):
-            load_scale_rows(nc.sync, plane, dram, first)
-            load_scale_rows(nc.sync, plane, dram, first + 1)
-
         nc.sync.dma_start(out=x8_raw[:], in_=x8.rearrange("(p i) t -> p (i t)", i=PACK))
-        two_scale_loads(w4_s_raw, w4_scales, 0)
+        load_x4_scale_rows(0)
+        load_w4_scale_rows(0)
         nc.sync.dma_start(out=w8_raw[:], in_=w8.rearrange("(p i) n -> p (i n)", i=PACK))
-        two_scale_loads(w4_s_raw, w4_scales, 2)
+        load_x4_scale_rows(1)
+        load_w4_scale_rows(1)
         nc.sync.dma_start(out=w4_w_raw[:].bitcast(I32), in_=w4_words.rearrange("g p b -> p g b").bitcast(I32))
-        two_scale_loads(x4_s, x4_scales, 0)
+        load_w4_scale_rows(2)
+        load_w4_scale_rows(3)
         nc.sync.dma_start(out=x4_w[:].bitcast(I32), in_=x4_words.rearrange("g p b -> p g b").bitcast(I32))
-        two_scale_loads(x4_s, x4_scales, 2)
         for a in range(GROUPS):
             nc.sync.dma_start(out=res[a][:], in_=rows_of(r, a))
 
         interleave("scalar", x8_bf[1], x8_raw, 1)
         interleave("vector", x8_bf[0], x8_raw, 0)
-        quantize_x8(0)
-        quantize_x8(1)
+        for h in range(HALVES):
+            quantize(x8_c[h][:], x8_s[h][:], x8_bf[h][:])
 
         order = [(h, j) for j in range(PACK) for h in range(HALVES)]
         deal_w8("vector", 0, 0)
         deal_w8("scalar", 0, 1)
         quantize_w8(0, 0)
-        deal_w4_words(0)
+        for g in range(PASSES4):
+            spread_x4_scale_rows(g)
         quantize_w8(0, 1)
         for h, j in order:
             fp8_pass(0, h, j)
+        deal_w4_words(0)
         deal_w4_scales(0)
         for h, j in order:
             fp4_passes(0, h, j)
@@ -202,41 +216,21 @@ def tile_mix_atom_fm_pl_res_kernel(
             quantize_w8(a, 0)
             quantize_w8(a, 1)
 
-        def adds_and_next_passes(a, steps):
-            for h, j in steps:
+        last = GROUPS - 1
+        for a in range(GROUPS):
+            for step, (h, j) in enumerate(order, start=1):
                 add_residual(a, h, j)
-                if a + 1 < GROUPS:
+                if a < last:
                     fp8_pass(a + 1, h, j)
                     fp4_passes(a + 1, h, j)
-
-        def adds_with_interleave(a):
-            adds_and_next_passes(a, order[:-1])
-            interleave("scalar", res_bf[a][0], res[a], 0)
-            adds_and_next_passes(a, order[-1:])
-
-        adds_with_interleave(0)
-        interleave("scalar", res_bf[0][1], res[0], 1)
-        store_res(0)
-        adds_and_next_passes(1, order[:5])
-        quantize_res(0, 0)
-        adds_and_next_passes(1, order[5:7])
-        interleave("scalar", res_bf[1][0], res[1], 0)
-        adds_and_next_passes(1, order[7:])
-        interleave("scalar", res_bf[1][1], res[1], 1)
-        store_res(1)
-        quantize_res(0, 1)
-        store_codes(0)
-        adds_and_next_passes(2, order[:4])
-        quantize_res(1, 0)
-        adds_and_next_passes(2, order[4:6])
-        quantize_res(1, 1)
-        store_codes(1)
-        adds_and_next_passes(2, order[6:7])
-        interleave("scalar", res_bf[2][0], res[2], 0)
-        adds_and_next_passes(2, order[7:])
-        store_res(2)
-        interleave("vector", res_bf[2][1], res[2], 1)
-        quantize_res(2, 1)
-        quantize_res(2, 0)
-        store_codes(2)
+                if j == PACK - 1:
+                    interleave("vector" if (a, h) == (last, 1) else "scalar", res_bf[a][h], res[a], h)
+                if a > 0 and step in QUANTISE_AFTER:
+                    quantize_res(a - 1, QUANTISE_AFTER.index(step))
+                if a > 0 and step == QUANTISE_AFTER[-1]:
+                    store_codes(a - 1)
+            store_res(a)
+        quantize_res(last, 1)
+        quantize_res(last, 0)
+        store_codes(last)
         store_scales()

@@ -42,7 +42,7 @@ def tile_mix_atom_fm_pl_res_kernel(
         x8_raw = sb("x8_raw", [P, PACK * T], F32)
         w8_raw = sb("w8_raw", [P, PACK * M], F32)
         x4_w = sb("x4_w", [P, PASSES4, 2 * T], U8)
-        x4_s = sb("x4_s", [P, PASSES4 * 2 * T], U8)
+        x4_s = sb("x4_s", [P, 5 * T], U8)
         w4_w_raw = sb("w4_w_raw", [P, PASSES4, 2 * M], U8)
         w4_s_raw = sb("w4_s_raw", [P, PASSES4, M], U8)
         w4_w = [sb(f"w4_w{a}", [P, PASSES4, PACK, 2 * P], U8) for a in range(GROUPS)]
@@ -57,7 +57,7 @@ def tile_mix_atom_fm_pl_res_kernel(
         res_bf = [[sb(f"res_bf{a}_{h}", [P, PACK * N], BF16) for h in range(HALVES)] for a in range(GROUPS)]
         out_c = [sb(f"out_c{a}", [P, T], U32) for a in range(GROUPS)]
         planes = sb("planes", [P, T], U8)
-        out_s = [planes[PACK * (a + 1) : P, :] for a in range(GROUPS)]
+        out_s = [planes[PACK * a : P, :] for a in range(GROUPS)]
         banks = {}
 
         def rows_of(dram, a):
@@ -122,7 +122,7 @@ def tile_mix_atom_fm_pl_res_kernel(
 
         def fp4_passes(a, h, j):
             for g in range(PASSES4):
-                first = (2 * g + 1) * T + N * h
+                first = g * T + N * h
                 nc.tensor.matmul_mx(
                     out=banks[a, h, j][:],
                     lhsT=w4_w[a][:, g, j, :].bitcast(FP4X4),
@@ -141,18 +141,21 @@ def tile_mix_atom_fm_pl_res_kernel(
             by_row = w4_scales.rearrange("g (q s) n -> s q g n", s=4)
             nc.sync.dma_start(out=w4_s_raw[s:P:QUAD].bitcast(I32), in_=by_row[s].bitcast(I32))
 
-        def load_x4_scale_rows(odd):
-            by_parity = x4_scales.rearrange("g (u o s) n -> o s (g u) n", o=2, s=4)
-            first = (2 + odd) * QUAD
+        def load_x4_scale_rows_direct(s):
+            by_row = x4_scales[0].rearrange("(q s) n -> s q n", s=4)
+            nc.sync.dma_start(out=x4_s[s:P:QUAD, 0:T].bitcast(I32), in_=by_row[s].bitcast(I32))
+
+        def load_x4_scale_rows_staged(s):
+            by_row = x4_scales[1].rearrange("(q s) n -> s q n", s=4)
             nc.sync.dma_start(
-                out=x4_s[first : first + 4, :].rearrange("s (c n) -> s c n", n=T).bitcast(I32),
-                in_=by_parity[odd].bitcast(I32),
+                out=x4_s[s : s + 2, T : 5 * T].rearrange("s (q n) -> s q n", n=T).bitcast(I32),
+                in_=by_row[s : s + 2].bitcast(I32),
             )
 
-        def spread_x4_scale_rows(g):
+        def spread_x4_scale_rows(q):
             nc.vector.tensor_copy(
-                out=x4_s[0 : P // 2, (2 * g + 1) * T : (2 * g + 2) * T].bitcast(I32),
-                in_=x4_s[P // 2 : P, 2 * g * T : (2 * g + 1) * T].bitcast(I32),
+                out=x4_s[QUAD * q : QUAD * q + 4, T : 2 * T].bitcast(I32),
+                in_=x4_s[0:4, (q + 1) * T : (q + 2) * T].bitcast(I32),
             )
 
         def store_codes(a):
@@ -166,19 +169,21 @@ def tile_mix_atom_fm_pl_res_kernel(
                 queue = nc.sync if q < 2 else nc.scalar
                 queue.dma_start(
                     out=out_2[:, 4 * q : 4 * q + 4, :].bitcast(I32),
-                    in_=planes[QUAD * q + PACK : QUAD * q + PACK * (GROUPS + 1), :].bitcast(I32),
+                    in_=planes[QUAD * q : QUAD * q + PACK * GROUPS, :].bitcast(I32),
                 )
 
         def store_res(a):
             nc.sync.dma_start(out=rows_of(out_0, a), in_=res[a][:])
 
-        nc.vector.memset(x4_s[:].bitcast(I32), 0)
+        nc.vector.memset(x4_s[:, 0 : 2 * T].bitcast(I32), 0)
         nc.vector.memset(w4_s_raw[:].rearrange("p g n -> p (g n)").bitcast(I32), 0)
         nc.sync.dma_start(out=x8_raw[:], in_=x8.rearrange("(p i) t -> p (i t)", i=PACK))
-        load_x4_scale_rows(0)
-        load_w4_scale_rows(0)
+        load_x4_scale_rows_staged(0)
+        load_x4_scale_rows_staged(2)
+        for s in range(4):
+            load_x4_scale_rows_direct(s)
         nc.sync.dma_start(out=w8_raw[:], in_=w8.rearrange("(p i) n -> p (i n)", i=PACK))
-        load_x4_scale_rows(1)
+        load_w4_scale_rows(0)
         load_w4_scale_rows(1)
         nc.sync.dma_start(out=w4_w_raw[:].bitcast(I32), in_=w4_words.rearrange("g p b -> p g b").bitcast(I32))
         load_w4_scale_rows(2)
@@ -191,13 +196,13 @@ def tile_mix_atom_fm_pl_res_kernel(
         interleave("vector", x8_bf[0], x8_raw, 0)
         for h in range(HALVES):
             quantize(x8_c[h][:], x8_s[h][:], x8_bf[h][:])
+        for q in range(1, 4):
+            spread_x4_scale_rows(q)
 
         order = [(h, j) for j in range(PACK) for h in range(HALVES)]
         deal_w8("vector", 0, 0)
         deal_w8("scalar", 0, 1)
         quantize_w8(0, 0)
-        for g in range(PASSES4):
-            spread_x4_scale_rows(g)
         quantize_w8(0, 1)
         for h, j in order:
             fp8_pass(0, h, j)

@@ -42,7 +42,7 @@ def tile_mix_atom_fm_pl_res_kernel(
         x8_raw = sb("x8_raw", [P, PACK * T], F32)
         w8_raw = sb("w8_raw", [P, PACK * M], F32)
         x4_w = sb("x4_w", [P, PASSES4, 2 * T], U8)
-        x4_s = sb("x4_s", [P, 5 * T], U8)
+        x4_s = sb("x4_s", [P, PASSES4, T], U8)
         w4_w_raw = sb("w4_w_raw", [P, PASSES4, 2 * M], U8)
         w4_s_raw = sb("w4_s_raw", [P, PASSES4, M], U8)
         w4_w = [sb(f"w4_w{a}", [P, PASSES4, PACK, 2 * P], U8) for a in range(GROUPS)]
@@ -122,13 +122,12 @@ def tile_mix_atom_fm_pl_res_kernel(
 
         def fp4_passes(a, h, j):
             for g in range(PASSES4):
-                first = g * T + N * h
                 nc.tensor.matmul_mx(
                     out=banks[a, h, j][:],
                     lhsT=w4_w[a][:, g, j, :].bitcast(FP4X4),
                     lhsT_scale=w4_s[a][:, g, j, :],
                     rhs=x4_w[:, g, 2 * N * h : 2 * N * (h + 1)].bitcast(FP4X4),
-                    rhs_scale=x4_s[:, first : first + N],
+                    rhs_scale=x4_s[:, g, N * h : N * (h + 1)],
                     start=False,
                     stop=(g == PASSES4 - 1),
                 )
@@ -137,25 +136,11 @@ def tile_mix_atom_fm_pl_res_kernel(
             part = res[a][:, j * T + h * N : j * T + (h + 1) * N]
             nc.vector.tensor_tensor(out=part, in0=banks[a, h, j][:], in1=part, op=ADD)
 
-        def load_w4_scale_rows(s):
-            by_row = w4_scales.rearrange("g (q s) n -> s q g n", s=4)
-            nc.sync.dma_start(out=w4_s_raw[s:P:QUAD].bitcast(I32), in_=by_row[s].bitcast(I32))
-
-        def load_x4_scale_rows_direct(s):
-            by_row = x4_scales[0].rearrange("(q s) n -> s q n", s=4)
-            nc.sync.dma_start(out=x4_s[s:P:QUAD, 0:T].bitcast(I32), in_=by_row[s].bitcast(I32))
-
-        def load_x4_scale_rows_staged(s):
-            by_row = x4_scales[1].rearrange("(q s) n -> s q n", s=4)
+        def load_scale_rows(plane, dram, s, first=0, step=1):
+            by_row = dram.rearrange("g (q s) n -> s q g n", s=4)
             nc.sync.dma_start(
-                out=x4_s[s : s + 2, T : 5 * T].rearrange("s (q n) -> s q n", n=T).bitcast(I32),
-                in_=by_row[s : s + 2].bitcast(I32),
-            )
-
-        def spread_x4_scale_rows(q):
-            nc.vector.tensor_copy(
-                out=x4_s[QUAD * q : QUAD * q + 4, T : 2 * T].bitcast(I32),
-                in_=x4_s[0:4, (q + 1) * T : (q + 2) * T].bitcast(I32),
+                out=plane[QUAD * first + s : P : QUAD * step].bitcast(I32),
+                in_=by_row[s, first::step].bitcast(I32),
             )
 
         def store_codes(a):
@@ -175,19 +160,18 @@ def tile_mix_atom_fm_pl_res_kernel(
         def store_res(a):
             nc.sync.dma_start(out=rows_of(out_0, a), in_=res[a][:])
 
-        nc.vector.memset(x4_s[:, 0 : 2 * T].bitcast(I32), 0)
+        nc.vector.memset(x4_s[:].rearrange("p g n -> p (g n)").bitcast(I32), 0)
         nc.vector.memset(w4_s_raw[:].rearrange("p g n -> p (g n)").bitcast(I32), 0)
         nc.sync.dma_start(out=x8_raw[:], in_=x8.rearrange("(p i) t -> p (i t)", i=PACK))
-        load_x4_scale_rows_staged(0)
-        load_x4_scale_rows_staged(2)
         for s in range(4):
-            load_x4_scale_rows_direct(s)
+            load_scale_rows(x4_s, x4_scales, s)
+        load_scale_rows(w4_s_raw, w4_scales, 0)
         nc.sync.dma_start(out=w8_raw[:], in_=w8.rearrange("(p i) n -> p (i n)", i=PACK))
-        load_w4_scale_rows(0)
-        load_w4_scale_rows(1)
+        load_scale_rows(w4_s_raw, w4_scales, 3, first=0, step=2)
+        load_scale_rows(w4_s_raw, w4_scales, 3, first=1, step=2)
         nc.sync.dma_start(out=w4_w_raw[:].bitcast(I32), in_=w4_words.rearrange("g p b -> p g b").bitcast(I32))
-        load_w4_scale_rows(2)
-        load_w4_scale_rows(3)
+        load_scale_rows(w4_s_raw, w4_scales, 1)
+        load_scale_rows(w4_s_raw, w4_scales, 2)
         nc.sync.dma_start(out=x4_w[:].bitcast(I32), in_=x4_words.rearrange("g p b -> p g b").bitcast(I32))
         for a in range(GROUPS):
             nc.sync.dma_start(out=res[a][:], in_=rows_of(r, a))
@@ -196,8 +180,6 @@ def tile_mix_atom_fm_pl_res_kernel(
         interleave("vector", x8_bf[0], x8_raw, 0)
         for h in range(HALVES):
             quantize(x8_c[h][:], x8_s[h][:], x8_bf[h][:])
-        for q in range(1, 4):
-            spread_x4_scale_rows(q)
 
         order = [(h, j) for j in range(PACK) for h in range(HALVES)]
         deal_w8("vector", 0, 0)

@@ -163,16 +163,18 @@ def tile_mix_atom_fm_pl_res_kernel(
         nc.vector.memset(x4_s[:].rearrange("p g n -> p (g n)").bitcast(I32), 0)
         nc.vector.memset(w4_s_raw[:].rearrange("p g n -> p (g n)").bitcast(I32), 0)
         nc.sync.dma_start(out=x8_raw[:], in_=x8.rearrange("(p i) t -> p (i t)", i=PACK))
-        for s in range(4):
-            load_scale_rows(x4_s, x4_scales, s)
-        load_scale_rows(w4_s_raw, w4_scales, 0)
-        nc.sync.dma_start(out=w8_raw[:], in_=w8.rearrange("(p i) n -> p (i n)", i=PACK))
+        load_scale_rows(x4_s, x4_scales, 0)
+        load_scale_rows(x4_s, x4_scales, 1)
         load_scale_rows(w4_s_raw, w4_scales, 3, first=0, step=2)
+        nc.sync.dma_start(out=w8_raw[:], in_=w8.rearrange("(p i) n -> p (i n)", i=PACK))
+        load_scale_rows(w4_s_raw, w4_scales, 0)
         load_scale_rows(w4_s_raw, w4_scales, 3, first=1, step=2)
         nc.sync.dma_start(out=w4_w_raw[:].bitcast(I32), in_=w4_words.rearrange("g p b -> p g b").bitcast(I32))
         load_scale_rows(w4_s_raw, w4_scales, 1)
         load_scale_rows(w4_s_raw, w4_scales, 2)
         nc.sync.dma_start(out=x4_w[:].bitcast(I32), in_=x4_words.rearrange("g p b -> p g b").bitcast(I32))
+        load_scale_rows(x4_s, x4_scales, 2)
+        load_scale_rows(x4_s, x4_scales, 3)
         for a in range(GROUPS):
             nc.sync.dma_start(out=res[a][:], in_=rows_of(r, a))
 

from contextlib import ExitStack

import concourse.mybir as mybir

O, K4, M, T = 512, 1024, 1536, 1024
FLOPS = 2 * (O + K4) * M * T

F32 = mybir.dt.float32
BF16 = mybir.dt.bfloat16
I32 = mybir.dt.int32
U32 = mybir.dt.uint32
U16 = mybir.dt.uint16
U8 = mybir.dt.uint8
FP8X4 = mybir.dt.float8_e4m3fn_x4
FP4X4 = mybir.dt.float4_e2m1fn_x4
ADD = mybir.AluOpType.add

P = 128
PACK = 4
SPAN = P * PACK
N = 512
QUAD = 32
GROUPS = M // SPAN
HALVES = T // N
PASSES4 = K4 // SPAN
ALIGN = 256
QUANTISE_AFTER = (4, 7)


def tile_mix_atom_fm_pl_res_kernel(
    tc, x8, w8, x4_words, x4_scales, w4_words, w4_scales, r, out_0, out_1, out_2
):
    nc = tc.nc
    with ExitStack() as ctx:
        keep = ctx.enter_context(tc.tile_pool(name="keep", bufs=1))
        psum = ctx.enter_context(tc.psum_pool(name="psum", bufs=1))
        ctx.enter_context(tc.manual_schedule())

        def sb(name, shape, dtype):
            return keep.tile(shape, dtype, name=name, align_bytes=ALIGN)

        x8_raw = sb("x8_raw", [P, PACK * T], F32)
        w8_raw = sb("w8_raw", [P, PACK * M], F32)
        x4_w = sb("x4_w", [P, PASSES4, 2 * T], U8)
        x4_s = sb("x4_s", [P, PASSES4, T], U8)
        w4_w_raw = sb("w4_w_raw", [P, PASSES4, 2 * M], U8)
        w4_s_raw = sb("w4_s_raw", [P, PASSES4, M], U8)
        w4_w = [sb(f"w4_w{a}", [P, PASSES4, PACK, 2 * P], U8) for a in range(GROUPS)]
        w4_s = [sb(f"w4_s{a}", [P, PASSES4, PACK, P], U8) for a in range(GROUPS)]
        x8_bf = [sb(f"x8_bf{h}", [P, PACK * N], BF16) for h in range(HALVES)]
        x8_c = [sb(f"x8_c{h}", [P, N], U32) for h in range(HALVES)]
        x8_s = [sb(f"x8_s{h}", [P, N], U8) for h in range(HALVES)]
        w8_bf = [[sb(f"w8_bf{a}_{u}", [P, 2 * SPAN], BF16) for u in range(2)] for a in range(GROUPS)]
        w8_c = [[sb(f"w8_c{a}_{u}", [P, 2 * P], U32) for u in range(2)] for a in range(GROUPS)]
        w8_s = [[sb(f"w8_s{a}_{u}", [P, 2 * P], U8) for u in range(2)] for a in range(GROUPS)]
        res = [sb(f"res{a}", [P, PACK * T], F32) for a in range(GROUPS)]
        res_bf = [[sb(f"res_bf{a}_{h}", [P, PACK * N], BF16) for h in range(HALVES)] for a in range(GROUPS)]
        out_c = [sb(f"out_c{a}", [P, T], U32) for a in range(GROUPS)]
        planes = sb("planes", [P, T], U8)
        out_s = [planes[PACK * a : P, :] for a in range(GROUPS)]
        banks = {}

        def rows_of(dram, a):
            return dram[a * SPAN : (a + 1) * SPAN, :].rearrange("(p j) t -> p (j t)", j=PACK)

        def copy_on(engine, out, in_):
            if engine == "vector":
                nc.vector.tensor_copy(out=out, in_=in_)
            else:
                nc.scalar.copy(out=out, in_=in_)

        def interleave(engine, dst, src, h):
            rows = src[:].rearrange("p (i t) -> p i t", i=PACK)
            copy_on(
                engine,
                dst[:].rearrange("p (c e i) -> p c i e", e=4, i=PACK),
                rows[:, :, h * N : (h + 1) * N].rearrange("p i (c e) -> p c i e", e=4),
            )

        def deal_w8(engine, a, u):
            rows = w8_raw[:].rearrange("p (i n) -> p i n", i=PACK)
            copy_on(
                engine,
                w8_bf[a][u][:].rearrange("p (v m i) -> p m i v", v=2, i=PACK),
                rows[:, :, a * SPAN : (a + 1) * SPAN].rearrange("p i (m u v) -> p u m i v", u=2, v=2)[:, u],
            )

        def deal_w4_words(a):
            nc.vector.tensor_copy(
                out=w4_w[a][:].bitcast(U16),
                in_=w4_w_raw[:].bitcast(U16)[:, :, SPAN * a : SPAN * (a + 1)].rearrange("p g (m j) -> p g j m", j=PACK),
            )

        def deal_w4_scales(a):
            nc.vector.tensor_copy(
                out=w4_s[a][:],
                in_=w4_s_raw[:, :, SPAN * a : SPAN * (a + 1)].rearrange("p g (m j) -> p g j m", j=PACK),
            )

        def quantize(codes, scales, values):
            nc.vector.quantize_mx(out=codes.bitcast(FP8X4), scales=scales, in_=values)

        def quantize_w8(a, u):
            quantize(w8_c[a][u][:], w8_s[a][u][:], w8_bf[a][u][:])

        def quantize_res(a, h):
            cols = slice(h * N, (h + 1) * N)
            quantize(out_c[a][:, cols], out_s[a][:, cols], res_bf[a][h][:])

        def fp8_pass(a, h, j):
            u, v = divmod(j, 2)
            banks[a, h, j] = psum.tile([P, N], F32, name=f"bank{h}_{j}")
            nc.tensor.matmul_mx(
                out=banks[a, h, j][:],
                lhsT=w8_c[a][u][:, v * P : (v + 1) * P].bitcast(FP8X4),
                lhsT_scale=w8_s[a][u][:, v * P : (v + 1) * P],
                rhs=x8_c[h][:].bitcast(FP8X4),
                rhs_scale=x8_s[h][:],
                start=True,
                stop=False,
            )

        def fp4_passes(a, h, j):
            for g in range(PASSES4):
                nc.tensor.matmul_mx(
                    out=banks[a, h, j][:],
                    lhsT=w4_w[a][:, g, j, :].bitcast(FP4X4),
                    lhsT_scale=w4_s[a][:, g, j, :],
                    rhs=x4_w[:, g, 2 * N * h : 2 * N * (h + 1)].bitcast(FP4X4),
                    rhs_scale=x4_s[:, g, N * h : N * (h + 1)],
                    start=False,
                    stop=(g == PASSES4 - 1),
                )

        def add_residual(a, h, j):
            part = res[a][:, j * T + h * N : j * T + (h + 1) * N]
            nc.vector.tensor_tensor(out=part, in0=banks[a, h, j][:], in1=part, op=ADD)

        def load_scale_rows(plane, dram, s, first=0, step=1):
            by_row = dram.rearrange("g (q s) n -> s q g n", s=4)
            nc.sync.dma_start(
                out=plane[QUAD * first + s : P : QUAD * step].bitcast(I32),
                in_=by_row[s, first::step].bitcast(I32),
            )

        def store_codes(a):
            nc.sync.dma_start(
                out=out_1[a].rearrange("p t b -> p (t b)").bitcast(I32),
                in_=out_c[a][:].bitcast(I32),
            )

        def store_scales():
            for q in range(4):
                queue = nc.sync if q < 2 else nc.scalar
                queue.dma_start(
                    out=out_2[:, 4 * q : 4 * q + 4, :].bitcast(I32),
                    in_=planes[QUAD * q : QUAD * q + PACK * GROUPS, :].bitcast(I32),
                )

        def store_res(a):
            nc.sync.dma_start(out=rows_of(out_0, a), in_=res[a][:])

        nc.vector.memset(x4_s[:].rearrange("p g n -> p (g n)").bitcast(I32), 0)
        nc.vector.memset(w4_s_raw[:].rearrange("p g n -> p (g n)").bitcast(I32), 0)
        nc.sync.dma_start(out=x8_raw[:], in_=x8.rearrange("(p i) t -> p (i t)", i=PACK))
        load_scale_rows(x4_s, x4_scales, 0)
        load_scale_rows(x4_s, x4_scales, 1)
        load_scale_rows(w4_s_raw, w4_scales, 3, first=0, step=2)
        nc.sync.dma_start(out=w8_raw[:], in_=w8.rearrange("(p i) n -> p (i n)", i=PACK))
        load_scale_rows(w4_s_raw, w4_scales, 0)
        load_scale_rows(w4_s_raw, w4_scales, 3, first=1, step=2)
        nc.sync.dma_start(out=w4_w_raw[:].bitcast(I32), in_=w4_words.rearrange("g p b -> p g b").bitcast(I32))
        load_scale_rows(w4_s_raw, w4_scales, 1)
        load_scale_rows(w4_s_raw, w4_scales, 2)
        nc.sync.dma_start(out=x4_w[:].bitcast(I32), in_=x4_words.rearrange("g p b -> p g b").bitcast(I32))
        load_scale_rows(x4_s, x4_scales, 2)
        load_scale_rows(x4_s, x4_scales, 3)
        for a in range(GROUPS):
            nc.sync.dma_start(out=res[a][:], in_=rows_of(r, a))

        interleave("scalar", x8_bf[1], x8_raw, 1)
        interleave("vector", x8_bf[0], x8_raw, 0)
        for h in range(HALVES):
            quantize(x8_c[h][:], x8_s[h][:], x8_bf[h][:])

        order = [(h, j) for j in range(PACK) for h in range(HALVES)]
        deal_w8("vector", 0, 0)
        deal_w8("scalar", 0, 1)
        quantize_w8(0, 0)
        quantize_w8(0, 1)
        for h, j in order:
            fp8_pass(0, h, j)
        deal_w4_words(0)
        deal_w4_scales(0)
        for h, j in order:
            fp4_passes(0, h, j)
        deal_w8("vector", 1, 0)
        deal_w8("scalar", 1, 1)
        deal_w8("scalar", 2, 0)
        deal_w8("scalar", 2, 1)
        for a in range(1, GROUPS):
            deal_w4_words(a)
            deal_w4_scales(a)
        for a in range(1, GROUPS):
            quantize_w8(a, 0)
            quantize_w8(a, 1)

        last = GROUPS - 1
        for a in range(GROUPS):
            for step, (h, j) in enumerate(order, start=1):
                add_residual(a, h, j)
                if a < last:
                    fp8_pass(a + 1, h, j)
                    fp4_passes(a + 1, h, j)
                if j == PACK - 1:
                    interleave("vector" if (a, h) == (last, 1) else "scalar", res_bf[a][h], res[a], h)
                if a > 0 and step in QUANTISE_AFTER:
                    quantize_res(a - 1, QUANTISE_AFTER.index(step))
                if a > 0 and step == QUANTISE_AFTER[-1]:
                    store_codes(a - 1)
            store_res(a)
        quantize_res(last, 1)
        quantize_res(last, 0)
        store_codes(last)
        store_scales()
